import numpy as np
import ml_dtypes


def mxq(x, axis, fmt="e4m3"):
    dtype, down = {"e4m3": (ml_dtypes.float8_e4m3fn, 7), "e5m2": (ml_dtypes.float8_e5m2, 14)}[fmt]
    v = np.moveaxis(np.asarray(x, np.float32).astype(ml_dtypes.bfloat16).astype(np.float64), axis, -1)
    blocks = v.reshape(v.shape[:-1] + (-1, 32))
    amax = np.abs(blocks).max(-1, keepdims=True)
    byte = np.maximum(np.where(amax > 0, np.frexp(amax)[1] - 1 + 127, 0) - down, 1)
    scale = np.exp2(byte - 127.0)
    codes = (blocks / scale).astype(np.float32).astype(dtype).astype(np.float64)
    return np.moveaxis((codes * scale).reshape(v.shape), -1, axis)


WIDE = False


def mx_kscale(k):
    if not WIDE:
        return np.ones(k)
    levels = np.array([10, -10, 5, -5, 0])
    if k % 512:
        return np.exp2(np.random.permutation(np.resize(levels, k // 32))).repeat(32)
    a = np.empty((k // 512, 16))
    for p in range(k // 512):
        a[p, :8] = np.random.permutation(np.resize(levels, 8))
        for g in range(8):
            far = levels[np.abs(levels - a[p, g]) >= 10]
            a[p, g + 8] = far[np.random.randint(len(far))]
    return np.exp2(a.ravel()).repeat(32)


BF16 = ml_dtypes.bfloat16


def bf(x):
    return np.asarray(x, np.float32).astype(BF16)


def f64(x):
    return np.asarray(x).astype(np.float64)


B, N, M, D = 6, 1024, 512, 512


def softmax(x):
    e = np.exp(x - x.max(axis=-1, keepdims=True))
    return e / e.sum(axis=-1, keepdims=True)


def aggregate(b1, g1, v):
    p1 = softmax(f64(b1)) * f64(g1)[None, :]
    return mxq(p1, 1, "e4m3") @ mxq(f64(v), 1, "e4m3")


def broadcast(q, a, g2, u):
    s2 = (mxq(f64(q), 2, "e4m3") @ mxq(f64(a).transpose(0, 2, 1), 1, "e4m3")) / np.sqrt(D)
    p2 = softmax(s2) * f64(g2)[None, None, :]
    return mxq(p2, 2, "e4m3") @ mxq(u, 1, "e4m3")


def draw0():
    s, r, t = mx_kscale(D), mx_kscale(N), mx_kscale(M)
    q = bf(np.random.standard_normal((B, N, D)) * s)
    a = bf(np.random.standard_normal((B, M, D)) / s)
    v = bf(np.random.standard_normal((B, N, D)) / r[:, None])
    b1 = bf(np.random.standard_normal((M, N)))
    g1 = bf(np.random.standard_normal(N) * np.sqrt(N) * r)
    g2 = bf(np.random.standard_normal(M) * np.sqrt(M) * t)
    g3 = bf((1.0 + 0.1 * np.random.standard_normal(M)) / t)
    return {"q": q, "a": a, "v": v, "b1": b1, "g1": g1, "g2": g2, "g3": g3}


def core(q, a, v, b1, g1, g2, g3):
    t = aggregate(b1, g1, v)
    u = f64(g3)[None, :, None] * t
    y = broadcast(q, a, g2, u)
    return y


def e4m3fn_bytes(y):
    return np.clip(np.asarray(y, np.float64), -448.0, 448.0).astype(np.float32).astype(ml_dtypes.float8_e4m3fn).view(np.uint8)


def e4m3fn_values(b):
    return np.asarray(b, np.uint8).view(ml_dtypes.float8_e4m3fn).astype(np.float64)


def setup_inputs():
    d = draw0()
    x0 = np.asarray(d['v']).astype(np.float64)
    s = (np.max(np.abs(x0), axis=(0, 2), keepdims=True) / 448.0).astype(np.float32)
    out = {}
    for k, v in d.items():
        if k == 'v':
            out['v_bytes'] = e4m3fn_bytes(x0 / s.astype(np.float64))
            out['v_scale'] = s
        else:
            out[k] = v
    return out


def reference(q, a, v_bytes, v_scale, b1, g1, g2, g3):
    return core(q, a, e4m3fn_values(v_bytes) * v_scale.astype(np.float64), b1, g1, g2, g3)

@@ -1,0 +1,492 @@
+from contextlib import ExitStack
+
+import concourse.mybir as mybir
+from concourse.masks import make_identity
+
+B, N, M, D = 6, 1024, 512, 512
+FLOPS = 3 * 2 * B * N * M * D
+
+F32 = mybir.dt.float32
+BF16 = mybir.dt.bfloat16
+U32 = mybir.dt.uint32
+U8 = mybir.dt.uint8
+FP8 = mybir.dt.float8_e4m3fn
+X4 = mybir.dt.float8_e4m3fn_x4
+ALU = mybir.AluOpType
+ACT = mybir.ActivationFunctionType
+AX = mybir.AxisListType
+
+P = 128
+INV = 1.0 / (512.0**0.5)
+NBANK = 6
+PAIRS = N // (2 * P)
+STEPS = B * PAIRS
+
+
+def tile_agentattentionbiased_t_kernel(tc, q, a, v_bytes, v_scale, b1, g1, g2, g3, out):
+    nc = tc.nc
+    with ExitStack() as ctx:
+        const = ctx.enter_context(tc.tile_pool(name="const", bufs=1))
+        pool = ctx.enter_context(tc.tile_pool(name="work", bufs=2))
+        psum = ctx.enter_context(tc.psum_pool(name="psum", bufs=2))
+        ctx.enter_context(tc.manual_schedule())
+
+        def sb(tag, shape, dtype, bufs):
+            return pool.tile(shape, dtype, name=tag, tag=tag, bufs=bufs, align_bytes=64)
+
+        def ps(tag, shape, dtype, bufs):
+            return psum.tile(shape, dtype, name=tag, tag=tag, bufs=bufs)
+
+        def keep(tag, shape, dtype):
+            return const.tile(shape, dtype, name=tag, tag=tag, align_bytes=64)
+
+        state = {}
+
+        def load_a(b):
+            t = sb("a_rows", [P, 4, D], BF16, 2)
+            nc.sync.dma_start(out=t[:], in_=a[b].rearrange("(j p) d -> p j d", p=P))
+            state["a", b] = t
+
+        def load_q(b, pieces):
+            t = sb("q_rows", [P, 8, D], BF16, 3)
+            src = q[b].rearrange("(p j) d -> p j d", j=8)
+            state["q", b] = t
+            for lo, hi in pieces:
+                nc.sync.dma_start(out=t[:, lo:hi, :], in_=src[:, lo:hi, :])
+
+        def load_v(b):
+            t = sb("v_raw", [P, 2, 4, D], U8, 3)
+            nc.sync.dma_start(
+                out=t[:].rearrange("p g t d -> p g (t d)"),
+                in_=v_bytes[b].rearrange("(g p t) d -> p g (t d)", g=2, t=4),
+            )
+            state["vb", b] = t
+
+        warm = keep("warm", [P, 1], F32)
+        nc.vector.memset(warm[:], 0.0)
+        warm2 = keep("warm2", [P, 1], F32)
+        nc.scalar.activation(warm2[:], warm[:], ACT.Exp)
+
+        load_a(0)
+        load_q(0, [(0, 4)])
+        sc = keep("v_scales", [P, 2, 4], F32)
+        nc.scalar.dma_start(out=sc[:], in_=v_scale.rearrange("o (g p t) x -> p (o g) (t x)", g=2, t=4))
+        g3b = keep("g3_rows", [P, 4], BF16)
+        nc.scalar.dma_start(out=g3b[:], in_=g3.rearrange("(p t) -> p t", t=4))
+        b1_sb = keep("b1_rows", [P, 4, N], BF16)
+        b1_src = b1.rearrange("(m t) n -> m t n", t=4)
+        for h in range(2):
+            nc.sync.dma_start(out=b1_sb[:, 2 * h : 2 * h + 2, :], in_=b1_src[:, 2 * h : 2 * h + 2, :])
+        g2n = keep("g2_nat", [P, M], BF16)
+        nc.sync.dma_start(out=g2n[:], in_=g2.partition_broadcast(P))
+        load_v(0)
+        g1b = keep("g1_all", [P, N], BF16)
+        nc.sync.dma_start(out=g1b[:], in_=g1.partition_broadcast(P))
+        nc.sync.dma_start(
+            out=state["q", 0][:, 4:8, :], in_=q[0].rearrange("(p j) d -> p j d", j=8)[:, 4:8, :]
+        )
+        load_v(1)
+        load_a(1)
+        load_q(1, [(0, 4), (4, 8)])
+        load_v(2)
+
+        ident = keep("ident", [P, P], F32)
+        make_identity(nc, ident[:])
+        ident16 = keep("ident16", [P, P], BF16)
+        nc.vector.tensor_copy(out=ident16[:], in_=ident[:])
+        perm = keep("perm", [P, P], F32)
+        nc.vector.tensor_copy(
+            out=perm[:].rearrange("p (u h e) -> p u h e", u=2, e=2),
+            in_=ident[:].rearrange("p (h u e) -> p u h e", u=2, e=2),
+        )
+        g2b = keep("g2_all", [P, M], BF16)
+
+        def tr_q(k):
+            b, i = divmod(k, PAIRS)
+            words = state["q", b][:].rearrange("p j d -> p (j d)").bitcast(F32)
+            x = ps("b", [P, 2, 2, P], F32, NBANK)
+            for j in range(2):
+                base = (2 * i + j) * (D // 2)
+                for u in range(2):
+                    nc.tensor.transpose(x[:, j, u, :], words[:, base + u : base + D // 2 : 2], ident[:])
+            state["trq", k] = x
+
+        def words4(t):
+            return t[:].rearrange("p j r t -> p (j r t)").bitcast(F32).rearrange("p (j r u) -> p j r u", j=2, u=2)
+
+        def cp_q(k):
+            g = sb("qg", [P, 2, P, 4], BF16, 3)
+            nc.scalar.copy(out=words4(g), in_=state["trq", k][:].rearrange("p j u r -> p j r u"))
+            state["qg", k] = g
+
+        def quant(dst, dsc, src):
+            nc.vector.quantize_mx(out=dst.bitcast(X4), scales=dsc, in_=src)
+
+        def qz_q(k):
+            c = sb("qc", [P, 2 * P], U32, 2)
+            s = sb("qs", [P, 2 * P], U8, 2)
+            quant(c[:], s[:], state["qg", k][:].rearrange("p j r t -> p (j r t)"))
+            state["qc", k] = (c, s)
+
+        def tr_a(b, h):
+            words = state["a", b][:].rearrange("p j d -> p (j d)").bitcast(F32)
+            x = ps("b", [P, 2, 2, P], F32, NBANK)
+            for j in range(2):
+                base = (2 * h + j) * (D // 2)
+                for u in range(2):
+                    nc.tensor.transpose(x[:, j, u, :], words[:, base + u : base + D // 2 : 2], perm[:])
+            state["tra", b, h] = x
+
+        def cp_a(b, h, eng):
+            if h == 0:
+                state["ag", b] = sb("ag", [P, 2, 2, P, 4], BF16, 2)
+            g = state["ag", b]
+            gw = g[:].rearrange("p u h r t -> p (u h r t)").bitcast(F32)
+            gw = gw.rearrange("p (u h j r w) -> p u h j r w", u=2, h=2, j=2, w=2)
+            x = state["tra", b, h][:].rearrange("p j w (u r) -> p u j r w", u=2)
+            for u in range(2):
+                eng(out=gw[:, u, h], in_=x[:, u])
+
+        def qz_a(b):
+            c = sb("ac", [P, M], U32, 2)
+            s = sb("as", [P, M], U8, 2)
+            quant(c[:], s[:], state["ag", b][:].rearrange("p u h r t -> p (u h r t)"))
+            state["ac", b] = (c, s)
+
+        def widen(b, i, eng):
+            if i == 0:
+                state["vw", b] = sb("vw", [P, 2, 4, D], BF16, 2)
+            g, t = divmod(i, 4)
+            src = state["vb", b][:, g, t, :].bitcast(FP8)
+            dst = state["vw", b][:, g, t, :]
+            if eng == "v":
+                nc.vector.tensor_scalar(out=dst, in0=src, scalar1=sc[:, g, t : t + 1], scalar2=None, op0=ALU.mult)
+            else:
+                nc.scalar.activation(dst, src, ACT.Copy, scale=sc[:, g, t : t + 1])
+
+        def mm_v(b, c):
+            x = ps("b", [P, 2, P, 4], BF16, NBANK)
+            for g in range(2):
+                nc.tensor.matmul(
+                    x[:, g],
+                    lhsT=ident16[:],
+                    rhs=state["vw", b][:, g, :, c * P : (c + 1) * P].rearrange("p t d -> p d t"),
+                    start=True,
+                    stop=True,
+                )
+            state["vx", b, c] = x
+
+        def cp_v(b, c):
+            g = sb("vg", [P, 2, P, 4], BF16, 3)
+            nc.scalar.copy(
+                out=g[:].rearrange("p g d t -> p (g d t)"),
+                in_=state["vx", b, c][:].rearrange("p g d t -> p (g d t)"),
+            )
+            state["vg", b, c] = g
+
+        def qz_v(b, c):
+            w = sb("vc", [P, 2, P], U32, 4)
+            s = sb("vs", [P, 2, P], U8, 4)
+            quant(
+                w[:].rearrange("p g d -> p (g d)"),
+                s[:].rearrange("p g d -> p (g d)"),
+                state["vg", b, c][:].rearrange("p g d t -> p (g d t)"),
+            )
+            state["vc", b, c] = (w, s)
+
+        def mx(dst, l, r, lsl, rsl, start=True, stop=True):
+            nc.tensor.matmul_mx(
+                dst,
+                lhsT=l[0][lsl].bitcast(X4),
+                lhsT_scale=l[1][lsl],
+                rhs=r[0][rsl].bitcast(X4),
+                rhs_scale=r[1][rsl],
+                start=start,
+                stop=stop,
+            )
+
+        ALL = slice(None)
+
+        def mm_1(b, c):
+            x = ps("b", [P, 4, P], F32, NBANK)
+            for t in range(4):
+                for g in range(2):
+                    mx(x[:, t, :], state["p1c"], state["vc", b, c], (ALL, t, g, ALL), (ALL, g, ALL), g == 0, g == 1)
+            state["ux", b, c] = x
+
+        def tt_u(b, c):
+            g = sb("ug", [P, P, 4], BF16, 2)
+            nc.vector.tensor_tensor(
+                out=g[:],
+                in0=state["ux", b, c][:].rearrange("p t d -> p d t"),
+                in1=g3b[:].unsqueeze(1).to_broadcast([P, P, 4]),
+                op=ALU.mult,
+            )
+            state["ug", b, c] = g
+
+        def qz_u(b, c):
+            if c == 0:
+                state["uc", b] = (sb("uc", [P, D], U32, 2), sb("us", [P, D], U8, 2))
+            w, s = state["uc", b]
+            cols = slice(c * P, (c + 1) * P)
+            quant(w[:, cols], s[:, cols], state["ug", b, c][:].rearrange("p d t -> p (d t)"))
+
+        def mm_2(k):
+            b = k // PAIRS
+            xs = []
+            for j in range(2):
+                x = ps("s2", [P, M], F32, 2)
+                mx(x[:], state["qc", k], state["ac", b], (ALL, slice(j * P, (j + 1) * P)), (ALL, ALL))
+                xs.append(x)
+            state["s2", k] = xs
+
+        def maxes(k):
+            m = [sb("mx", [P, 1], F32, 4) for j in range(2)]
+            n = [sb("nb", [P, 1], F32, 4) for j in range(2)]
+            for j in range(2):
+                nc.vector.tensor_reduce(out=m[j][:], in_=state["s2", k][j][:], axis=AX.X, op=ALU.max)
+                nc.gpsimd.tensor_scalar(
+                    out=n[j][:], in0=m[j][:], scalar1=-INV, scalar2=0.0, op0=ALU.mult, op1=ALU.add
+                )
+            state["nb", k] = n
+
+        def exps(k):
+            e = sb("e", [P, 2, M], F32, 2)
+            s = sb("sum", [P, 2], F32, 3)
+            for j in range(2):
+                nc.scalar.activation(
+                    e[:, j, :],
+                    state["s2", k][j][:],
+                    ACT.Exp,
+                    bias=state["nb", k][j][:],
+                    scale=INV,
+                    accum_out=s[:, j : j + 1],
+                )
+            state["e", k] = (e, s)
+
+        def norm(k):
+            e, s = state["e", k]
+            r = sb("rs", [P, 2], F32, 3)
+            nc.vector.reciprocal(out=r[:], in_=s[:])
+            p2 = sb("p2", [P, 2, M], BF16, 2)
+            for j in range(2):
+                nc.vector.scalar_tensor_tensor(
+                    out=p2[:, j, :], in0=e[:, j, :], scalar=r[:, j : j + 1], in1=g2b[:], op0=ALU.mult, op1=ALU.mult
+                )
+            state["p2", k] = p2
+
+        def tr_p(k):
+            words = state["p2", k][:].rearrange("p j m -> p (j m)").bitcast(F32)
+            x = ps("b", [P, 2, 2, P], F32, NBANK)
+            for j in range(2):
+                for u in range(2):
+                    lo = (2 * j + u) * P
+                    nc.tensor.transpose(x[:, j, u, :], words[:, lo : lo + P], ident[:])
+            state["trp", k] = x
+
+        def cp_p(k):
+            g = sb("p2g", [P, 2, P, 4], BF16, 2)
+            nc.scalar.copy(out=words4(g), in_=state["trp", k][:].rearrange("p j u r -> p j r u"))
+            state["p2g", k] = g
+
+        def qz_p(k):
+            c = sb("p2c", [P, 2 * P], U32, 2)
+            s = sb("p2s", [P, 2 * P], U8, 2)
+            quant(c[:], s[:], state["p2g", k][:].rearrange("p j r t -> p (j r t)"))
+            state["p2c", k] = (c, s)
+
+        def mm_3(k):
+            b = k // PAIRS
+            xs = []
+            for j in range(2):
+                x = ps("b", [P, D], F32, NBANK)
+                mx(x[:], state["p2c", k], state["uc", b], (ALL, slice(j * P, (j + 1) * P)), (ALL, ALL))
+                xs.append(x)
+            state["ox", k] = xs
+
+        def outs(k):
+            b, i = divmod(k, PAIRS)
+            o = sb("o_sb", [P, 2, D], F32, 3)
+            for j in range(2):
+                nc.scalar.copy(out=o[:, j, :], in_=state["ox", k][j][:])
+            nc.sync.dma_start(out=out[b].rearrange("(p j) d -> p j d", j=8)[:, 2 * i : 2 * i + 2, :], in_=o[:])
+
+        tr_a(0, 0)
+        cp_a(0, 0, nc.scalar.copy)
+        tr_a(0, 1)
+        cp_a(0, 1, nc.vector.tensor_copy)
+        tr_q(0)
+        cp_q(0)
+        tr_q(1)
+        cp_q(1)
+        qz_a(0)
+        qz_q(0)
+        mm_2(0)
+        maxes(0)
+        exps(0)
+        f1 = sb("f1", [P, 4, 512], BF16, 1)
+        f2 = sb("f2", [P, 4, 256], BF16, 1)
+        f3 = sb("f3", [P, 4, 128], BF16, 1)
+        nm1 = keep("nm1", [P, 4], F32)
+        mx1 = keep("mx1", [P, 4], F32)
+        sum1 = keep("sum1", [P, 4], F32)
+        r1 = keep("r1", [P, 4], F32)
+        p1c = (keep("p1c", [P, 4, 2, P], U32), keep("p1s", [P, 4, 2, P], U8))
+        state["p1c"] = p1c
+
+        def p1_max(h):
+            hs = slice(2 * h, 2 * h + 2)
+            nc.vector.tensor_tensor(out=f1[:, hs, :], in0=b1_sb[:, hs, 0:512], in1=b1_sb[:, hs, 512:1024], op=ALU.max)
+            nc.vector.tensor_tensor(out=f2[:, hs, :], in0=f1[:, hs, 0:256], in1=f1[:, hs, 256:512], op=ALU.max)
+            nc.vector.tensor_tensor(out=f3[:, hs, :], in0=f2[:, hs, 0:128], in1=f2[:, hs, 128:256], op=ALU.max)
+            nc.vector.tensor_reduce(out=mx1[:, hs], in_=f3[:, hs, :], axis=AX.X, op=ALU.max)
+            nc.gpsimd.tensor_scalar(out=nm1[:, hs], in0=mx1[:, hs], scalar1=-1.0, scalar2=0.0, op0=ALU.mult, op1=ALU.add)
+
+        def p1_exp(t):
+            e1 = sb("e1", [P, N], F32, 2)
+            nc.scalar.activation(e1[:], b1_sb[:, t, :], ACT.Exp, bias=nm1[:, t : t + 1], accum_out=sum1[:, t : t + 1])
+            state["e1", t] = e1
+
+        def p1_norm(t):
+            nc.vector.reciprocal(out=r1[:, t : t + 1], in_=sum1[:, t : t + 1])
+            p1 = sb("p1", [P, N], BF16, 2)
+            nc.vector.scalar_tensor_tensor(
+                out=p1[:], in0=state["e1", t][:], scalar=r1[:, t : t + 1], in1=g1b[:], op0=ALU.mult, op1=ALU.mult
+            )
+            state["p1", t] = p1
+
+        def p1_tr(t):
+            words = state["p1", t][:].bitcast(F32)
+            x = ps("b", [P, 2, 2, P], F32, NBANK)
+            for g in range(2):
+                for u in range(2):
+                    nc.tensor.transpose(x[:, g, u, :], words[:, 256 * g + u : 256 * (g + 1) : 2], ident[:])
+            state["p1x", t] = x
+
+        def p1_cp(t):
+            pg = sb("p1g", [P, 2, P, 4], BF16, 2)
+            nc.scalar.copy(out=words4(pg), in_=state["p1x", t][:].rearrange("p g u r -> p g r u"))
+            state["p1g", t] = pg
+
+        def p1_qz(t):
+            quant(
+                p1c[0][:, t].rearrange("p g m -> p (g m)"),
+                p1c[1][:, t].rearrange("p g m -> p (g m)"),
+                state["p1g", t][:].rearrange("p g r t -> p (g r t)"),
+            )
+
+
+        p1_max(0)
+        p1_exp(0)
+        p1_max(1)
+        p1_exp(1)
+        nc.vector.tensor_copy(
+            out=g2b[:].rearrange("p (u h e) -> p u h e", u=2, e=2),
+            in_=g2n[:].rearrange("p (h u e) -> p u h e", u=2, e=2),
+        )
+        norm(0)
+        for w in range(4):
+            widen(0, w, "s" if w % 2 else "v")
+        p1_exp(2)
+        p1_norm(0)
+        p1_tr(0)
+        p1_exp(3)
+        p1_norm(1)
+        p1_tr(1)
+        p1_cp(0)
+        for w in range(4, 8):
+            widen(0, w, "s" if w % 2 else "v")
+        p1_qz(0)
+        p1_cp(1)
+        p1_norm(2)
+        mm_v(0, 0)
+        cp_v(0, 0)
+        p1_tr(2)
+        mm_v(0, 1)
+        p1_qz(1)
+        p1_norm(3)
+        p1_cp(2)
+        p1_tr(3)
+        qz_v(0, 0)
+        cp_v(0, 1)
+        p1_qz(2)
+        p1_cp(3)
+        mm_v(0, 2)
+        cp_v(0, 2)
+        qz_v(0, 1)
+        widen(1, 0, "v")
+        widen(1, 1, "v")
+        p1_qz(3)
+        mm_v(0, 3)
+        cp_v(0, 3)
+        mm_1(0, 0)
+        mm_1(0, 1)
+        widen(1, 2, "v")
+        widen(1, 3, "s")
+        qz_v(0, 2)
+        mm_1(0, 2)
+        tt_u(0, 0)
+        widen(1, 4, "v")
+        widen(1, 5, "s")
+        tt_u(0, 1)
+        qz_u(0, 0)
+        widen(1, 6, "v")
+        widen(1, 7, "s")
+        qz_v(0, 3)
+        tt_u(0, 2)
+        qz_u(0, 1)
+
+        for k in range(STEPS + 1):
+            b, i = divmod(k, PAIRS)
+            if i == 0 and b + 2 < B:
+                load_a(b + 2)
+                load_q(b + 2, [(0, 4), (4, 8)])
+            if i == 0 and b + 3 < B:
+                load_v(b + 3)
+            unit = k + 3
+            ub, uc = divmod(unit, PAIRS)
+            live = ub < B
+            if 1 <= k < STEPS:
+                maxes(k)
+            if k >= 1:
+                tr_p(k - 1)
+                cp_p(k - 1)
+            if k + 2 < STEPS:
+                tr_q(k + 2)
+            if i in (1, 2) and b + 1 < B:
+                tr_a(b + 1, i - 1)
+            if unit + 1 < B * PAIRS:
+                mm_v(*divmod(unit + 1, PAIRS))
+            if unit - 1 < B * PAIRS:
+                qz_u(*divmod(unit - 1, PAIRS))
+            if k >= 1:
+                qz_p(k - 1)
+                mm_3(k - 1)
+            if 1 <= k < STEPS:
+                exps(k)
+            if unit + 1 < B * PAIRS:
+                cp_v(*divmod(unit + 1, PAIRS))
+            if k + 1 < STEPS:
+                qz_q(k + 1)
+            if live and k >= 1:
+                qz_v(ub, uc)
+            if live:
+                mm_1(ub, uc)
+            if i == 3 and b + 1 < B:
+                qz_a(b + 1)
+            if k + 1 < STEPS:
+                mm_2(k + 1)
+            wp = [0, 3, 5, 7, 8]
+            if b + 2 < B:
+                for w in range(wp[i], wp[i + 1]):
+                    widen(b + 2, w, "v")
+            if 1 <= k < STEPS:
+                norm(k)
+            if k >= 1:
+                outs(k - 1)
+            if k + 2 < STEPS:
+                cp_q(k + 2)
+            if i in (1, 2) and b + 1 < B:
+                cp_a(b + 1, i - 1, nc.scalar.copy)
+            if live:
+                tt_u(ub, uc)

@@ -18,7 +18,10 @@ AX = mybir.AxisListType
 
 P = 128
 INV = 1.0 / (512.0**0.5)
-NBANK = 6
+NBANK = 5
+DELTA = 2
+ENGS = ("vv", "vv", "vv", "vv")
+L3 = 1 + DELTA
 PAIRS = N // (2 * P)
 STEPS = B * PAIRS
 
@@ -88,7 +91,6 @@ def tile_agentattentionbiased_t_kernel(tc, q, a, v_bytes, v_scale, b1, g1, g2, g
         load_v(1)
         load_a(1)
         load_q(1, [(0, 4), (4, 8)])
-        load_v(2)
 
         ident = keep("ident", [P, P], F32)
         make_identity(nc, ident[:])
@@ -226,54 +228,48 @@ def tile_agentattentionbiased_t_kernel(tc, q, a, v_bytes, v_scale, b1, g1, g2, g
 
         def qz_u(b, c):
             if c == 0:
-                state["uc", b] = (sb("uc", [P, D], U32, 2), sb("us", [P, D], U8, 2))
+                state["uc", b] = (sb("uc", [P, D], U32, 3), sb("us", [P, D], U8, 3))
             w, s = state["uc", b]
             cols = slice(c * P, (c + 1) * P)
             quant(w[:, cols], s[:, cols], state["ug", b, c][:].rearrange("p d t -> p (d t)"))
 
-        def mm_2(k):
-            b = k // PAIRS
-            xs = []
-            for j in range(2):
-                x = ps("s2", [P, M], F32, 2)
-                mx(x[:], state["qc", k], state["ac", b], (ALL, slice(j * P, (j + 1) * P)), (ALL, ALL))
-                xs.append(x)
-            state["s2", k] = xs
+        def mm_2(n):
+            k, j = divmod(n, 2)
+            x = ps("s2", [P, M], F32, 3)
+            mx(x[:], state["qc", k], state["ac", k // PAIRS], (ALL, slice(j * P, (j + 1) * P)), (ALL, ALL))
+            state["s2", n] = x
 
-        def maxes(k):
-            m = [sb("mx", [P, 1], F32, 4) for j in range(2)]
-            n = [sb("nb", [P, 1], F32, 4) for j in range(2)]
-            for j in range(2):
-                nc.vector.tensor_reduce(out=m[j][:], in_=state["s2", k][j][:], axis=AX.X, op=ALU.max)
-                nc.gpsimd.tensor_scalar(
-                    out=n[j][:], in0=m[j][:], scalar1=-INV, scalar2=0.0, op0=ALU.mult, op1=ALU.add
-                )
-            state["nb", k] = n
+        def maxes(n):
+            m = sb("mx", [P, 1], F32, 4)
+            nc.vector.tensor_reduce(out=m[:], in_=state["s2", n][:], axis=AX.X, op=ALU.max)
+            state["mx", n] = m
 
-        def exps(k):
-            e = sb("e", [P, 2, M], F32, 2)
-            s = sb("sum", [P, 2], F32, 3)
-            for j in range(2):
-                nc.scalar.activation(
-                    e[:, j, :],
-                    state["s2", k][j][:],
-                    ACT.Exp,
-                    bias=state["nb", k][j][:],
-                    scale=INV,
-                    accum_out=s[:, j : j + 1],
-                )
-            state["e", k] = (e, s)
+        def shift(n):
+            s = sb("nb", [P, 1], F32, 4)
+            nc.scalar.mul(s[:], state["mx", n][:], -INV)
+            state["nb", n] = s
 
-        def norm(k):
-            e, s = state["e", k]
-            r = sb("rs", [P, 2], F32, 3)
-            nc.vector.reciprocal(out=r[:], in_=s[:])
-            p2 = sb("p2", [P, 2, M], BF16, 2)
-            for j in range(2):
-                nc.vector.scalar_tensor_tensor(
-                    out=p2[:, j, :], in0=e[:, j, :], scalar=r[:, j : j + 1], in1=g2b[:], op0=ALU.mult, op1=ALU.mult
-                )
-            state["p2", k] = p2
+        def exps(n):
+            e = sb("e", [P, M], F32, 3)
+            s = sb("sum", [P, 1], F32, 4)
+            nc.scalar.activation(
+                e[:], state["s2", n][:], ACT.Exp, bias=state["nb", n][:], scale=INV, accum_out=s[:]
+            )
+            state["e", n] = (e, s)
+
+        def recip(n):
+            r = sb("rs", [P, 1], F32, 4)
+            nc.vector.reciprocal(out=r[:], in_=state["e", n][1][:])
+            state["rs", n] = r
+
+        def norm(n):
+            k, j = divmod(n, 2)
+            e, r = state["e", n][0], state["rs", n]
+            if j == 0:
+                state["p2", k] = sb("p2", [P, 2, M], BF16, 3)
+            nc.vector.scalar_tensor_tensor(
+                out=state["p2", k][:, j, :], in0=e[:], scalar=r[:], in1=g2b[:], op0=ALU.mult, op1=ALU.mult
+            )
 
         def tr_p(k):
             words = state["p2", k][:].rearrange("p j m -> p (j m)").bitcast(F32)
@@ -290,8 +286,8 @@ def tile_agentattentionbiased_t_kernel(tc, q, a, v_bytes, v_scale, b1, g1, g2, g
             state["p2g", k] = g
 
         def qz_p(k):
-            c = sb("p2c", [P, 2 * P], U32, 2)
-            s = sb("p2s", [P, 2 * P], U8, 2)
+            c = sb("p2c", [P, 2 * P], U32, 2 + DELTA)
+            s = sb("p2s", [P, 2 * P], U8, 2 + DELTA)
             quant(c[:], s[:], state["p2g", k][:].rearrange("p j r t -> p (j r t)"))
             state["p2c", k] = (c, s)
 
@@ -304,12 +300,16 @@ def tile_agentattentionbiased_t_kernel(tc, q, a, v_bytes, v_scale, b1, g1, g2, g
                 xs.append(x)
             state["ox", k] = xs
 
-        def outs(k):
+        def out_copy(k, j, eng):
+            if j == 0:
+                state["o", k] = sb("o_sb", [P, 2, D], F32, 4)
+            eng(out=state["o", k][:, j, :], in_=state["ox", k][j][:])
+
+        def store(k):
             b, i = divmod(k, PAIRS)
-            o = sb("o_sb", [P, 2, D], F32, 3)
-            for j in range(2):
-                nc.scalar.copy(out=o[:, j, :], in_=state["ox", k][j][:])
-            nc.sync.dma_start(out=out[b].rearrange("(p j) d -> p j d", j=8)[:, 2 * i : 2 * i + 2, :], in_=o[:])
+            nc.sync.dma_start(
+                out=out[b].rearrange("(p j) d -> p j d", j=8)[:, 2 * i : 2 * i + 2, :], in_=state["o", k][:]
+            )
 
         tr_a(0, 0)
         cp_a(0, 0, nc.scalar.copy)
@@ -322,7 +322,9 @@ def tile_agentattentionbiased_t_kernel(tc, q, a, v_bytes, v_scale, b1, g1, g2, g
         qz_a(0)
         qz_q(0)
         mm_2(0)
+        mm_2(1)
         maxes(0)
+        shift(0)
         exps(0)
         f1 = sb("f1", [P, 4, 512], BF16, 1)
         f2 = sb("f2", [P, 4, 256], BF16, 1)
@@ -376,6 +378,17 @@ def tile_agentattentionbiased_t_kernel(tc, q, a, v_bytes, v_scale, b1, g1, g2, g
             )
 
 
+        def v_unit(s):
+            n = s + 3 - DELTA
+            return divmod(n, PAIRS) if 0 <= n < B * PAIRS else None
+
+        def w_unit(s, engs):
+            n = s + 8 - DELTA
+            if 0 <= n < B * PAIRS:
+                b, i = divmod(n, PAIRS)
+                for w in range(2):
+                    widen(b, 2 * i + w, engs[w])
+
         p1_max(0)
         p1_exp(0)
         p1_max(1)
@@ -384,9 +397,8 @@ def tile_agentattentionbiased_t_kernel(tc, q, a, v_bytes, v_scale, b1, g1, g2, g
             out=g2b[:].rearrange("p (u h e) -> p u h e", u=2, e=2),
             in_=g2n[:].rearrange("p (h u e) -> p u h e", u=2, e=2),
         )
-        norm(0)
-        for w in range(4):
-            widen(0, w, "s" if w % 2 else "v")
+        for s in (DELTA - 8, DELTA - 7):
+            w_unit(s, "vs")
         p1_exp(2)
         p1_norm(0)
         p1_tr(0)
@@ -394,99 +406,106 @@ def tile_agentattentionbiased_t_kernel(tc, q, a, v_bytes, v_scale, b1, g1, g2, g
         p1_norm(1)
         p1_tr(1)
         p1_cp(0)
-        for w in range(4, 8):
-            widen(0, w, "s" if w % 2 else "v")
+        for s in (DELTA - 6, DELTA - 5):
+            w_unit(s, "vs")
         p1_qz(0)
         p1_cp(1)
         p1_norm(2)
         mm_v(0, 0)
-        cp_v(0, 0)
         p1_tr(2)
-        mm_v(0, 1)
         p1_qz(1)
         p1_norm(3)
         p1_cp(2)
         p1_tr(3)
-        qz_v(0, 0)
-        cp_v(0, 1)
+        cp_v(0, 0)
         p1_qz(2)
         p1_cp(3)
-        mm_v(0, 2)
-        cp_v(0, 2)
-        qz_v(0, 1)
-        widen(1, 0, "v")
-        widen(1, 1, "v")
-        p1_qz(3)
-        mm_v(0, 3)
-        cp_v(0, 3)
-        mm_1(0, 0)
-        mm_1(0, 1)
-        widen(1, 2, "v")
-        widen(1, 3, "s")
-        qz_v(0, 2)
-        mm_1(0, 2)
-        tt_u(0, 0)
-        widen(1, 4, "v")
-        widen(1, 5, "s")
-        tt_u(0, 1)
-        qz_u(0, 0)
-        widen(1, 6, "v")
-        widen(1, 7, "s")
-        qz_v(0, 3)
-        tt_u(0, 2)
-        qz_u(0, 1)
+        for s in range(DELTA - 4, 0):
+            w_unit(s, "vs")
+            if v_unit(s):
+                qz_v(*v_unit(s))
+            if s == DELTA - 3:
+                p1_qz(3)
+            if s > DELTA - 4:
+                mm_v(*v_unit(s + 1))
+                cp_v(*v_unit(s + 1))
+            if v_unit(s):
+                mm_1(*v_unit(s))
+                tt_u(*v_unit(s))
+            if s >= DELTA - 2:
+                qz_u(*v_unit(s - 1))
+        if DELTA == 3:
+            p1_qz(3)
 
-        for k in range(STEPS + 1):
+        for k in range(STEPS + L3):
             b, i = divmod(k, PAIRS)
+            main = k < STEPS
             if i == 0 and b + 2 < B:
                 load_a(b + 2)
                 load_q(b + 2, [(0, 4), (4, 8)])
-            if i == 0 and b + 3 < B:
-                load_v(b + 3)
-            unit = k + 3
-            ub, uc = divmod(unit, PAIRS)
-            live = ub < B
-            if 1 <= k < STEPS:
-                maxes(k)
-            if k >= 1:
+                load_v(b + 2)
+            unit = v_unit(k)
+            after = v_unit(k + 1)
+            before = v_unit(k - 1)
+            q_next = k + 2 if k + 2 < STEPS else None
+            a_half = (b + 1, i - 1) if i in (1, 2) and b + 1 < B else None
+            done = k - L3 if k >= L3 else None
+            late = k >= STEPS
+            if 1 <= k <= STEPS:
                 tr_p(k - 1)
+            if q_next:
+                tr_q(q_next)
+            if a_half:
+                tr_a(*a_half)
+            if main:
+                maxes(2 * k + 1)
+            if 1 <= k <= STEPS:
                 cp_p(k - 1)
-            if k + 2 < STEPS:
-                tr_q(k + 2)
-            if i in (1, 2) and b + 1 < B:
-                tr_a(b + 1, i - 1)
-            if unit + 1 < B * PAIRS:
-                mm_v(*divmod(unit + 1, PAIRS))
-            if unit - 1 < B * PAIRS:
-                qz_u(*divmod(unit - 1, PAIRS))
-            if k >= 1:
-                qz_p(k - 1)
-                mm_3(k - 1)
-            if 1 <= k < STEPS:
-                exps(k)
-            if unit + 1 < B * PAIRS:
-                cp_v(*divmod(unit + 1, PAIRS))
+            if main:
+                shift(2 * k + 1)
+            if unit and k >= 1 - (DELTA < 3) * 0 and ("vg", *unit) not in state:
+                cp_v(*unit)
+            if main:
+                recip(2 * k)
             if k + 1 < STEPS:
                 qz_q(k + 1)
-            if live and k >= 1:
-                qz_v(ub, uc)
-            if live:
-                mm_1(ub, uc)
-            if i == 3 and b + 1 < B:
-                qz_a(b + 1)
+                mm_2(2 * k + 2)
+                mm_2(2 * k + 3)
+            if before:
+                qz_u(*before)
+            if main:
+                norm(2 * k)
+                exps(2 * k + 1)
+            if q_next:
+                cp_q(q_next)
+            if 1 <= k <= STEPS:
+                qz_p(k - 1)
+            if unit and ("vc", *unit) not in state:
+                qz_v(*unit)
+            if done is not None:
+                mm_3(done)
+            if unit:
+                mm_1(*unit)
+            if after and ("vx", *after) not in state:
+                mm_v(*after)
+            if a_half:
+                cp_a(*a_half, nc.scalar.copy)
             if k + 1 < STEPS:
-                mm_2(k + 1)
-            wp = [0, 3, 5, 7, 8]
-            if b + 2 < B:
-                for w in range(wp[i], wp[i + 1]):
-                    widen(b + 2, w, "v")
-            if 1 <= k < STEPS:
-                norm(k)
-            if k >= 1:
-                outs(k - 1)
-            if k + 2 < STEPS:
-                cp_q(k + 2)
-            if i in (1, 2) and b + 1 < B:
-                cp_a(b + 1, i - 1, nc.scalar.copy)
-            if live:
-                tt_u(ub, uc)
+                maxes(2 * k + 2)
+                shift(2 * k + 2)
+            if done is not None:
+                out_copy(done, 0, nc.scalar.copy)
+            if main:
+                recip(2 * k + 1)
+            w_unit(k, ENGS[k % 4])
+            if main:
+                norm(2 * k + 1)
+            if k + 1 < STEPS:
+                exps(2 * k + 2)
+            if done is not None:
+                out_copy(done, 1, nc.vector.tensor_copy if late else nc.scalar.copy)
+                store(done)
+            if unit:
+                tt_u(*unit)
+            if i == 2 and b + 1 < B:
+                qz_a(b + 1)

@@ -20,7 +20,7 @@ P = 128
 INV = 1.0 / (512.0**0.5)
 NBANK = 5
 DELTA = 2
-ENGS = ("vv", "vv", "vv", "vv")
+ENGS = ("sv", "vv", "sv", "vv")
 L3 = 1 + DELTA
 PAIRS = N // (2 * P)
 STEPS = B * PAIRS
@@ -32,7 +32,7 @@ def tile_agentattentionbiased_t_kernel(tc, q, a, v_bytes, v_scale, b1, g1, g2, g
         const = ctx.enter_context(tc.tile_pool(name="const", bufs=1))
         pool = ctx.enter_context(tc.tile_pool(name="work", bufs=2))
         psum = ctx.enter_context(tc.psum_pool(name="psum", bufs=2))
-        ctx.enter_context(tc.manual_schedule())
+        ctx.enter_context(tc.manual_schedule(engines={mybir.EngineType.SP, mybir.EngineType.PE}))
 
         def sb(tag, shape, dtype, bufs):
             return pool.tile(shape, dtype, name=tag, tag=tag, bufs=bufs, align_bytes=64)
@@ -70,16 +70,16 @@ def tile_agentattentionbiased_t_kernel(tc, q, a, v_bytes, v_scale, b1, g1, g2, g
         warm2 = keep("warm2", [P, 1], F32)
         nc.scalar.activation(warm2[:], warm[:], ACT.Exp)
 
+        b1_sb = keep("b1_rows", [P, 4, N], BF16)
+        b1_src = b1.rearrange("(m t) n -> m t n", t=4)
+        nc.sync.dma_start(out=b1_sb[:, 0:2, :], in_=b1_src[:, 0:2, :])
         load_a(0)
         load_q(0, [(0, 4)])
+        nc.sync.dma_start(out=b1_sb[:, 2:4, :], in_=b1_src[:, 2:4, :])
         sc = keep("v_scales", [P, 2, 4], F32)
         nc.scalar.dma_start(out=sc[:], in_=v_scale.rearrange("o (g p t) x -> p (o g) (t x)", g=2, t=4))
         g3b = keep("g3_rows", [P, 4], BF16)
         nc.scalar.dma_start(out=g3b[:], in_=g3.rearrange("(p t) -> p t", t=4))
-        b1_sb = keep("b1_rows", [P, 4, N], BF16)
-        b1_src = b1.rearrange("(m t) n -> m t n", t=4)
-        for h in range(2):
-            nc.sync.dma_start(out=b1_sb[:, 2 * h : 2 * h + 2, :], in_=b1_src[:, 2 * h : 2 * h + 2, :])
         g2n = keep("g2_nat", [P, M], BF16)
         nc.sync.dma_start(out=g2n[:], in_=g2.partition_broadcast(P))
         load_v(0)
@@ -94,13 +94,13 @@ def tile_agentattentionbiased_t_kernel(tc, q, a, v_bytes, v_scale, b1, g1, g2, g
 
         ident = keep("ident", [P, P], F32)
         make_identity(nc, ident[:])
-        ident16 = keep("ident16", [P, P], BF16)
-        nc.vector.tensor_copy(out=ident16[:], in_=ident[:])
         perm = keep("perm", [P, P], F32)
-        nc.vector.tensor_copy(
+        nc.gpsimd.tensor_copy(
             out=perm[:].rearrange("p (u h e) -> p u h e", u=2, e=2),
             in_=ident[:].rearrange("p (h u e) -> p u h e", u=2, e=2),
         )
+        ident16 = keep("ident16", [P, P], BF16)
+        nc.gpsimd.tensor_copy(out=ident16[:], in_=ident[:])
         g2b = keep("g2_all", [P, M], BF16)
 
         def tr_q(k):
@@ -311,21 +311,6 @@ def tile_agentattentionbiased_t_kernel(tc, q, a, v_bytes, v_scale, b1, g1, g2, g
                 out=out[b].rearrange("(p j) d -> p j d", j=8)[:, 2 * i : 2 * i + 2, :], in_=state["o", k][:]
             )
 
-        tr_a(0, 0)
-        cp_a(0, 0, nc.scalar.copy)
-        tr_a(0, 1)
-        cp_a(0, 1, nc.vector.tensor_copy)
-        tr_q(0)
-        cp_q(0)
-        tr_q(1)
-        cp_q(1)
-        qz_a(0)
-        qz_q(0)
-        mm_2(0)
-        mm_2(1)
-        maxes(0)
-        shift(0)
-        exps(0)
         f1 = sb("f1", [P, 4, 512], BF16, 1)
         f2 = sb("f2", [P, 4, 256], BF16, 1)
         f3 = sb("f3", [P, 4, 128], BF16, 1)
@@ -336,21 +321,25 @@ def tile_agentattentionbiased_t_kernel(tc, q, a, v_bytes, v_scale, b1, g1, g2, g
         p1c = (keep("p1c", [P, 4, 2, P], U32), keep("p1s", [P, 4, 2, P], U8))
         state["p1c"] = p1c
 
+        def p1_fold(h, i):
+            hs = slice(2 * h, 2 * h + 2)
+            src, dst, w = ((b1_sb, f1, 512), (f1, f2, 256), (f2, f3, 128))[i]
+            nc.vector.tensor_tensor(out=dst[:, hs, :], in0=src[:, hs, 0:w], in1=src[:, hs, w : 2 * w], op=ALU.max)
+
         def p1_max(h):
             hs = slice(2 * h, 2 * h + 2)
-            nc.vector.tensor_tensor(out=f1[:, hs, :], in0=b1_sb[:, hs, 0:512], in1=b1_sb[:, hs, 512:1024], op=ALU.max)
-            nc.vector.tensor_tensor(out=f2[:, hs, :], in0=f1[:, hs, 0:256], in1=f1[:, hs, 256:512], op=ALU.max)
-            nc.vector.tensor_tensor(out=f3[:, hs, :], in0=f2[:, hs, 0:128], in1=f2[:, hs, 128:256], op=ALU.max)
             nc.vector.tensor_reduce(out=mx1[:, hs], in_=f3[:, hs, :], axis=AX.X, op=ALU.max)
-            nc.gpsimd.tensor_scalar(out=nm1[:, hs], in0=mx1[:, hs], scalar1=-1.0, scalar2=0.0, op0=ALU.mult, op1=ALU.add)
+            nc.scalar.mul(nm1[:, hs], mx1[:, hs], -1.0)
 
         def p1_exp(t):
             e1 = sb("e1", [P, N], F32, 2)
             nc.scalar.activation(e1[:], b1_sb[:, t, :], ACT.Exp, bias=nm1[:, t : t + 1], accum_out=sum1[:, t : t + 1])
             state["e1", t] = e1
 
-        def p1_norm(t):
+        def p1_recip(t):
             nc.vector.reciprocal(out=r1[:, t : t + 1], in_=sum1[:, t : t + 1])
+
+        def p1_norm(t):
             p1 = sb("p1", [P, N], BF16, 2)
             nc.vector.scalar_tensor_tensor(
                 out=p1[:], in0=state["e1", t][:], scalar=r1[:, t : t + 1], in1=g1b[:], op0=ALU.mult, op1=ALU.mult
@@ -387,55 +376,76 @@ def tile_agentattentionbiased_t_kernel(tc, q, a, v_bytes, v_scale, b1, g1, g2, g
             if 0 <= n < B * PAIRS:
                 b, i = divmod(n, PAIRS)
                 for w in range(2):
-                    widen(b, 2 * i + w, engs[w])
+                    if engs[w] != "-":
+                        widen(b, 2 * i + w, engs[w])
 
+        for i in range(3):
+            p1_fold(0, i)
         p1_max(0)
+        tr_a(0, 0)
+        cp_a(0, 0, nc.scalar.copy)
+        tr_a(0, 1)
+        cp_a(0, 1, nc.vector.tensor_copy)
+        tr_q(0)
+        cp_q(0)
         p1_exp(0)
-        p1_max(1)
+        qz_a(0)
+        p1_fold(1, 0)
+        qz_q(0)
+        mm_2(0)
+        mm_2(1)
+        p1_fold(1, 1)
         p1_exp(1)
-        nc.vector.tensor_copy(
+        p1_recip(0)
+        p1_fold(1, 2)
+        maxes(0)
+        p1_max(1)
+        p1_norm(0)
+        shift(0)
+        tr_q(1)
+        cp_q(1)
+        p1_tr(0)
+        exps(0)
+        nc.scalar.copy(
             out=g2b[:].rearrange("p (u h e) -> p u h e", u=2, e=2),
             in_=g2n[:].rearrange("p (h u e) -> p u h e", u=2, e=2),
         )
-        for s in (DELTA - 8, DELTA - 7):
-            w_unit(s, "vs")
+        p1_recip(1)
         p1_exp(2)
-        p1_norm(0)
-        p1_tr(0)
-        p1_exp(3)
+        widen(0, 0, "v")
+        p1_cp(0)
         p1_norm(1)
         p1_tr(1)
-        p1_cp(0)
-        for s in (DELTA - 6, DELTA - 5):
-            w_unit(s, "vs")
-        p1_qz(0)
-        p1_cp(1)
+        p1_exp(3)
+        widen(0, 1, "s")
+        p1_recip(2)
+        widen(0, 2, "v")
         p1_norm(2)
-        mm_v(0, 0)
+        widen(0, 3, "s")
+        p1_cp(1)
+        widen(0, 4, "v")
+        p1_recip(3)
+        p1_qz(0)
         p1_tr(2)
-        p1_qz(1)
         p1_norm(3)
+        widen(0, 5, "s")
+        widen(0, 6, "v")
         p1_cp(2)
+        widen(0, 7, "s")
+        p1_qz(1)
+        mm_v(0, 0)
         p1_tr(3)
-        cp_v(0, 0)
+        mm_v(0, 1)
         p1_qz(2)
+        cp_v(0, 0)
         p1_cp(3)
-        for s in range(DELTA - 4, 0):
-            w_unit(s, "vs")
-            if v_unit(s):
-                qz_v(*v_unit(s))
-            if s == DELTA - 3:
-                p1_qz(3)
-            if s > DELTA - 4:
-                mm_v(*v_unit(s + 1))
-                cp_v(*v_unit(s + 1))
-            if v_unit(s):
-                mm_1(*v_unit(s))
-                tt_u(*v_unit(s))
-            if s >= DELTA - 2:
-                qz_u(*v_unit(s - 1))
-        if DELTA == 3:
-            p1_qz(3)
+        cp_v(0, 1)
+        w_unit(DELTA - 4, "vv")
+        qz_v(0, 0)
+        p1_qz(3)
+        mm_1(0, 0)
+        w_unit(DELTA - 3, "vs")
+        tt_u(0, 0)
 
         for k in range(STEPS + L3):
             b, i = divmod(k, PAIRS)
@@ -490,6 +500,7 @@ def tile_agentattentionbiased_t_kernel(tc, q, a, v_bytes, v_scale, b1, g1, g2, g
                 mm_v(*after)
             if a_half:
                 cp_a(*a_half, nc.scalar.copy)
+            w_unit(k, ENGS[k % 4].replace("v", "-"))
             if k + 1 < STEPS:
                 maxes(2 * k + 2)
                 shift(2 * k + 2)
@@ -497,7 +508,7 @@ def tile_agentattentionbiased_t_kernel(tc, q, a, v_bytes, v_scale, b1, g1, g2, g
                 out_copy(done, 0, nc.scalar.copy)
             if main:
                 recip(2 * k + 1)
-            w_unit(k, ENGS[k % 4])
+            w_unit(k, ENGS[k % 4].replace("s", "-"))
             if main:
                 norm(2 * k + 1)
             if k + 1 < STEPS:

@@ -17,13 +17,16 @@ ACT = mybir.ActivationFunctionType
 AX = mybir.AxisListType
 
 P = 128
-INV = 1.0 / (512.0**0.5)
-NBANK = 5
-DELTA = 2
-ENGS = ("sv", "vv", "sv", "vv")
-L3 = 1 + DELTA
-PAIRS = N // (2 * P)
+PACK = 4
+INV_SQRT_D = 1.0 / (D**0.5)
+TILES = N // P
+PAIRS = TILES // 2
 STEPS = B * PAIRS
+CHUNKS = D // P
+BANKS = 5
+S2_BANKS = 3
+V_LAG = 2
+OUT_LAG = 1 + V_LAG
 
 
 def tile_agentattentionbiased_t_kernel(tc, q, a, v_bytes, v_scale, b1, g1, g2, g3, out):
@@ -32,65 +35,85 @@ def tile_agentattentionbiased_t_kernel(tc, q, a, v_bytes, v_scale, b1, g1, g2, g
         const = ctx.enter_context(tc.tile_pool(name="const", bufs=1))
         pool = ctx.enter_context(tc.tile_pool(name="work", bufs=2))
         psum = ctx.enter_context(tc.psum_pool(name="psum", bufs=2))
-        ctx.enter_context(tc.manual_schedule(engines={mybir.EngineType.SP, mybir.EngineType.PE}))
-
-        def sb(tag, shape, dtype, bufs):
-            return pool.tile(shape, dtype, name=tag, tag=tag, bufs=bufs, align_bytes=64)
-
-        def ps(tag, shape, dtype, bufs):
-            return psum.tile(shape, dtype, name=tag, tag=tag, bufs=bufs)
+        ctx.enter_context(tc.manual_schedule())
 
         def keep(tag, shape, dtype):
             return const.tile(shape, dtype, name=tag, tag=tag, align_bytes=64)
 
-        state = {}
+        def work(tag, shape, dtype, bufs):
+            return pool.tile(shape, dtype, name=tag, tag=tag, bufs=bufs, align_bytes=64)
+
+        def bank(shape, dtype):
+            return psum.tile(shape, dtype, name="bank", tag="bank", bufs=BANKS)
+
+        def mx_pair(tag, shape, bufs):
+            return work(tag + "_codes", shape, U32, bufs), work(tag + "_scales", shape, U8, bufs)
+
+        def quantize(dst, cols, src):
+            nc.vector.quantize_mx(out=dst[0][cols].bitcast(X4), scales=dst[1][cols], in_=src)
+
+        def multiply(dst, left, left_cols, right, right_cols, start=True, stop=True):
+            nc.tensor.matmul_mx(
+                dst,
+                lhsT=left[0][left_cols].bitcast(X4),
+                lhsT_scale=left[1][left_cols],
+                rhs=right[0][right_cols].bitcast(X4),
+                rhs_scale=right[1][right_cols],
+                start=start,
+                stop=stop,
+            )
+
+        def word_pairs(t):
+            return t.rearrange("p j r t -> p (j r t)").bitcast(F32).rearrange("p (j r u) -> p j r u", j=2, u=2)
+
+        ALL = slice(None)
+        live = {}
+
+        q_src = [q[b].rearrange("(p j) d -> p j d", j=TILES) for b in range(B)]
+        out_dst = [out[b].rearrange("(p j) d -> p j d", j=TILES) for b in range(B)]
 
         def load_a(b):
-            t = sb("a_rows", [P, 4, D], BF16, 2)
-            nc.sync.dma_start(out=t[:], in_=a[b].rearrange("(j p) d -> p j d", p=P))
-            state["a", b] = t
+            live["a", b] = work("a_rows", [P, M // P, D], BF16, 2)
+            nc.sync.dma_start(out=live["a", b][:], in_=a[b].rearrange("(j p) d -> p j d", p=P))
 
-        def load_q(b, pieces):
-            t = sb("q_rows", [P, 8, D], BF16, 3)
-            src = q[b].rearrange("(p j) d -> p j d", j=8)
-            state["q", b] = t
-            for lo, hi in pieces:
-                nc.sync.dma_start(out=t[:, lo:hi, :], in_=src[:, lo:hi, :])
+        def load_q(b, half):
+            if half == 0:
+                live["q", b] = work("q_rows", [P, TILES, D], BF16, 3)
+            tiles = slice(half * TILES // 2, (half + 1) * TILES // 2)
+            nc.sync.dma_start(out=live["q", b][:, tiles, :], in_=q_src[b][:, tiles, :])
 
         def load_v(b):
-            t = sb("v_raw", [P, 2, 4, D], U8, 3)
+            live["v bytes", b] = work("v_raw", [P, 2, PACK, D], U8, 3)
             nc.sync.dma_start(
-                out=t[:].rearrange("p g t d -> p g (t d)"),
-                in_=v_bytes[b].rearrange("(g p t) d -> p g (t d)", g=2, t=4),
+                out=live["v bytes", b][:].rearrange("p g t d -> p g (t d)"),
+                in_=v_bytes[b].rearrange("(g p t) d -> p g (t d)", g=2, t=PACK),
             )
-            state["vb", b] = t
 
-        warm = keep("warm", [P, 1], F32)
-        nc.vector.memset(warm[:], 0.0)
-        warm2 = keep("warm2", [P, 1], F32)
-        nc.scalar.activation(warm2[:], warm[:], ACT.Exp)
+        one = keep("one", [P, 1], F32)
+        nc.vector.memset(one[:], 0.0)
+        one_exp = keep("one_exp", [P, 1], F32)
+        nc.scalar.activation(one_exp[:], one[:], ACT.Exp)
 
-        b1_sb = keep("b1_rows", [P, 4, N], BF16)
-        b1_src = b1.rearrange("(m t) n -> m t n", t=4)
-        nc.sync.dma_start(out=b1_sb[:, 0:2, :], in_=b1_src[:, 0:2, :])
+        b1_rows = keep("b1_rows", [P, M // P, N], BF16)
+        b1_src = b1.rearrange("(m t) n -> m t n", t=PACK)
+        nc.sync.dma_start(out=b1_rows[:, 0:2, :], in_=b1_src[:, 0:2, :])
         load_a(0)
-        load_q(0, [(0, 4)])
-        nc.sync.dma_start(out=b1_sb[:, 2:4, :], in_=b1_src[:, 2:4, :])
-        sc = keep("v_scales", [P, 2, 4], F32)
-        nc.scalar.dma_start(out=sc[:], in_=v_scale.rearrange("o (g p t) x -> p (o g) (t x)", g=2, t=4))
-        g3b = keep("g3_rows", [P, 4], BF16)
-        nc.scalar.dma_start(out=g3b[:], in_=g3.rearrange("(p t) -> p t", t=4))
-        g2n = keep("g2_nat", [P, M], BF16)
-        nc.sync.dma_start(out=g2n[:], in_=g2.partition_broadcast(P))
+        load_q(0, 0)
+        nc.sync.dma_start(out=b1_rows[:, 2:4, :], in_=b1_src[:, 2:4, :])
+        v_factor = keep("v_factor", [P, 2, PACK], F32)
+        nc.scalar.dma_start(out=v_factor[:], in_=v_scale.rearrange("o (g p t) x -> p (o g) (t x)", g=2, t=PACK))
+        g3_cols = keep("g3_cols", [P, PACK], BF16)
+        nc.scalar.dma_start(out=g3_cols[:], in_=g3.rearrange("(p t) -> p t", t=PACK))
+        g2_plain = keep("g2_plain", [P, M], BF16)
+        nc.sync.dma_start(out=g2_plain[:], in_=g2.partition_broadcast(P))
         load_v(0)
-        g1b = keep("g1_all", [P, N], BF16)
-        nc.sync.dma_start(out=g1b[:], in_=g1.partition_broadcast(P))
-        nc.sync.dma_start(
-            out=state["q", 0][:, 4:8, :], in_=q[0].rearrange("(p j) d -> p j d", j=8)[:, 4:8, :]
-        )
+        g1_all = keep("g1_all", [P, N], BF16)
+        nc.sync.dma_start(out=g1_all[:], in_=g1.partition_broadcast(P))
+        load_q(0, 1)
         load_v(1)
         load_a(1)
-        load_q(1, [(0, 4), (4, 8)])
+        load_q(1, 0)
+        load_q(1, 1)
 
         ident = keep("ident", [P, P], F32)
         make_identity(nc, ident[:])
@@ -101,422 +124,405 @@ def tile_agentattentionbiased_t_kernel(tc, q, a, v_bytes, v_scale, b1, g1, g2, g
         )
         ident16 = keep("ident16", [P, P], BF16)
         nc.gpsimd.tensor_copy(out=ident16[:], in_=ident[:])
-        g2b = keep("g2_all", [P, M], BF16)
+        g2_all = keep("g2_all", [P, M], BF16)
 
-        def tr_q(k):
+        def turn(rows, first, identity):
+            words = rows[:].rearrange("p j d -> p (j d)").bitcast(F32)
+            x = bank([P, 2, 2, P], F32)
+            for j in range(2):
+                lo = (first + j) * (D // 2)
+                for u in range(2):
+                    nc.tensor.transpose(x[:, j, u, :], words[:, lo + u : lo + D // 2 : 2], identity[:])
+            return x
+
+        def q_turn(k):
             b, i = divmod(k, PAIRS)
-            words = state["q", b][:].rearrange("p j d -> p (j d)").bitcast(F32)
-            x = ps("b", [P, 2, 2, P], F32, NBANK)
-            for j in range(2):
-                base = (2 * i + j) * (D // 2)
-                for u in range(2):
-                    nc.tensor.transpose(x[:, j, u, :], words[:, base + u : base + D // 2 : 2], ident[:])
-            state["trq", k] = x
+            live["q turned", k] = turn(live["q", b], 2 * i, ident)
 
-        def words4(t):
-            return t[:].rearrange("p j r t -> p (j r t)").bitcast(F32).rearrange("p (j r u) -> p j r u", j=2, u=2)
+        def q_copy(k):
+            g = work("q_grouped", [P, 2, P, PACK], BF16, 3)
+            nc.scalar.copy(out=word_pairs(g[:]), in_=live["q turned", k][:].rearrange("p j u r -> p j r u"))
+            live["q grouped", k] = g
 
-        def cp_q(k):
-            g = sb("qg", [P, 2, P, 4], BF16, 3)
-            nc.scalar.copy(out=words4(g), in_=state["trq", k][:].rearrange("p j u r -> p j r u"))
-            state["qg", k] = g
+        def q_quantize(k):
+            live["q mx", k] = mx_pair("q", [P, 2 * P], 3)
+            quantize(live["q mx", k], (ALL, ALL), live["q grouped", k][:].rearrange("p j r t -> p (j r t)"))
 
-        def quant(dst, dsc, src):
-            nc.vector.quantize_mx(out=dst.bitcast(X4), scales=dsc, in_=src)
+        def a_turn(b, h):
+            live["a turned", b, h] = turn(live["a", b], 2 * h, perm)
 
-        def qz_q(k):
-            c = sb("qc", [P, 2 * P], U32, 2)
-            s = sb("qs", [P, 2 * P], U8, 2)
-            quant(c[:], s[:], state["qg", k][:].rearrange("p j r t -> p (j r t)"))
-            state["qc", k] = (c, s)
-
-        def tr_a(b, h):
-            words = state["a", b][:].rearrange("p j d -> p (j d)").bitcast(F32)
-            x = ps("b", [P, 2, 2, P], F32, NBANK)
-            for j in range(2):
-                base = (2 * h + j) * (D // 2)
-                for u in range(2):
-                    nc.tensor.transpose(x[:, j, u, :], words[:, base + u : base + D // 2 : 2], perm[:])
-            state["tra", b, h] = x
-
-        def cp_a(b, h, eng):
+        def a_copy(b, h, copy):
             if h == 0:
-                state["ag", b] = sb("ag", [P, 2, 2, P, 4], BF16, 2)
-            g = state["ag", b]
-            gw = g[:].rearrange("p u h r t -> p (u h r t)").bitcast(F32)
-            gw = gw.rearrange("p (u h j r w) -> p u h j r w", u=2, h=2, j=2, w=2)
-            x = state["tra", b, h][:].rearrange("p j w (u r) -> p u j r w", u=2)
+                live["a grouped", b] = work("a_grouped", [P, 2, 2, P, PACK], BF16, 2)
+            dst = live["a grouped", b][:].rearrange("p u h r t -> p (u h r t)").bitcast(F32)
+            dst = dst.rearrange("p (u h j r w) -> p u h j r w", u=2, h=2, j=2, w=2)
+            src = live["a turned", b, h][:].rearrange("p j w (u r) -> p u j r w", u=2)
             for u in range(2):
-                eng(out=gw[:, u, h], in_=x[:, u])
+                copy(out=dst[:, u, h], in_=src[:, u])
 
-        def qz_a(b):
-            c = sb("ac", [P, M], U32, 2)
-            s = sb("as", [P, M], U8, 2)
-            quant(c[:], s[:], state["ag", b][:].rearrange("p u h r t -> p (u h r t)"))
-            state["ac", b] = (c, s)
+        def a_quantize(b):
+            live["a mx", b] = mx_pair("a", [P, M], 2)
+            quantize(live["a mx", b], (ALL, ALL), live["a grouped", b][:].rearrange("p u h r t -> p (u h r t)"))
 
-        def widen(b, i, eng):
-            if i == 0:
-                state["vw", b] = sb("vw", [P, 2, 4, D], BF16, 2)
-            g, t = divmod(i, 4)
-            src = state["vb", b][:, g, t, :].bitcast(FP8)
-            dst = state["vw", b][:, g, t, :]
-            if eng == "v":
-                nc.vector.tensor_scalar(out=dst, in0=src, scalar1=sc[:, g, t : t + 1], scalar2=None, op0=ALU.mult)
+        def v_widen(b, w, engine):
+            if ("v wide", b) not in live:
+                live["v wide", b] = work("v_wide", [P, 2, PACK, D], BF16, 2)
+            g, t = divmod(w, PACK)
+            src = live["v bytes", b][:, g, t, :].bitcast(FP8)
+            dst = live["v wide", b][:, g, t, :]
+            factor = v_factor[:, g, t : t + 1]
+            if engine == "vector":
+                nc.vector.tensor_scalar(out=dst, in0=src, scalar1=factor, scalar2=None, op0=ALU.mult)
             else:
-                nc.scalar.activation(dst, src, ACT.Copy, scale=sc[:, g, t : t + 1])
+                nc.scalar.activation(dst, src, ACT.Copy, scale=factor)
 
-        def mm_v(b, c):
-            x = ps("b", [P, 2, P, 4], BF16, NBANK)
+        def v_interleave(b, c):
+            x = bank([P, 2, P, PACK], BF16)
             for g in range(2):
                 nc.tensor.matmul(
-                    x[:, g],
+                    x[:, g].rearrange("p d t -> p t d"),
                     lhsT=ident16[:],
-                    rhs=state["vw", b][:, g, :, c * P : (c + 1) * P].rearrange("p t d -> p d t"),
+                    rhs=live["v wide", b][:, g, :, c * P : (c + 1) * P],
                     start=True,
                     stop=True,
                 )
-            state["vx", b, c] = x
+            live["v bank", b, c] = x
 
-        def cp_v(b, c):
-            g = sb("vg", [P, 2, P, 4], BF16, 3)
+        def v_copy(b, c):
+            g = work("v_grouped", [P, 2, P, PACK], BF16, 3)
             nc.scalar.copy(
                 out=g[:].rearrange("p g d t -> p (g d t)"),
-                in_=state["vx", b, c][:].rearrange("p g d t -> p (g d t)"),
+                in_=live["v bank", b, c][:].rearrange("p g d t -> p (g d t)"),
             )
-            state["vg", b, c] = g
+            live["v grouped", b, c] = g
 
-        def qz_v(b, c):
-            w = sb("vc", [P, 2, P], U32, 4)
-            s = sb("vs", [P, 2, P], U8, 4)
-            quant(
-                w[:].rearrange("p g d -> p (g d)"),
-                s[:].rearrange("p g d -> p (g d)"),
-                state["vg", b, c][:].rearrange("p g d t -> p (g d t)"),
-            )
-            state["vc", b, c] = (w, s)
+        def v_quantize(b, c):
+            live["v mx", b, c] = mx_pair("v", [P, 2 * P], 4)
+            quantize(live["v mx", b, c], (ALL, ALL), live["v grouped", b, c][:].rearrange("p g d t -> p (g d t)"))
 
-        def mx(dst, l, r, lsl, rsl, start=True, stop=True):
-            nc.tensor.matmul_mx(
-                dst,
-                lhsT=l[0][lsl].bitcast(X4),
-                lhsT_scale=l[1][lsl],
-                rhs=r[0][rsl].bitcast(X4),
-                rhs_scale=r[1][rsl],
-                start=start,
-                stop=stop,
-            )
-
-        ALL = slice(None)
-
-        def mm_1(b, c):
-            x = ps("b", [P, 4, P], F32, NBANK)
-            for t in range(4):
+        def t_multiply(b, c):
+            x = bank([P, PACK, P], F32)
+            for t in range(PACK):
                 for g in range(2):
-                    mx(x[:, t, :], state["p1c"], state["vc", b, c], (ALL, t, g, ALL), (ALL, g, ALL), g == 0, g == 1)
-            state["ux", b, c] = x
+                    multiply(
+                        x[:, t, :], p1_mx, (ALL, t, g, ALL), live["v mx", b, c], (ALL, slice(g * P, (g + 1) * P)), g == 0, g == 1
+                    )
+            live["t bank", b, c] = x
 
-        def tt_u(b, c):
-            g = sb("ug", [P, P, 4], BF16, 2)
+        def u_scale(b, c):
+            g = work("u_grouped", [P, P, PACK], BF16, 2)
             nc.vector.tensor_tensor(
                 out=g[:],
-                in0=state["ux", b, c][:].rearrange("p t d -> p d t"),
-                in1=g3b[:].unsqueeze(1).to_broadcast([P, P, 4]),
+                in0=live["t bank", b, c][:].rearrange("p t d -> p d t"),
+                in1=g3_cols[:].unsqueeze(1).to_broadcast([P, P, PACK]),
                 op=ALU.mult,
             )
-            state["ug", b, c] = g
+            live["u grouped", b, c] = g
 
-        def qz_u(b, c):
+        def u_quantize(b, c):
             if c == 0:
-                state["uc", b] = (sb("uc", [P, D], U32, 3), sb("us", [P, D], U8, 3))
-            w, s = state["uc", b]
-            cols = slice(c * P, (c + 1) * P)
-            quant(w[:, cols], s[:, cols], state["ug", b, c][:].rearrange("p d t -> p (d t)"))
+                live["u mx", b] = mx_pair("u", [P, D], 3)
+            quantize(live["u mx", b], (ALL, slice(c * P, (c + 1) * P)), live["u grouped", b, c][:].rearrange("p d t -> p (d t)"))
 
-        def mm_2(n):
+        def s2_multiply(n):
             k, j = divmod(n, 2)
-            x = ps("s2", [P, M], F32, 3)
-            mx(x[:], state["qc", k], state["ac", k // PAIRS], (ALL, slice(j * P, (j + 1) * P)), (ALL, ALL))
-            state["s2", n] = x
+            x = psum.tile([P, M], F32, name="s2", tag="s2", bufs=S2_BANKS)
+            multiply(x[:], live["q mx", k], (ALL, slice(j * P, (j + 1) * P)), live["a mx", k // PAIRS], (ALL, ALL))
+            live["s2", n] = x
 
-        def maxes(n):
-            m = sb("mx", [P, 1], F32, 4)
-            nc.vector.tensor_reduce(out=m[:], in_=state["s2", n][:], axis=AX.X, op=ALU.max)
-            state["mx", n] = m
+        def s2_max(n):
+            live["max", n] = work("row_max", [P, 1], F32, 4)
+            nc.vector.tensor_reduce(out=live["max", n][:], in_=live["s2", n][:], axis=AX.X, op=ALU.max)
 
-        def shift(n):
-            s = sb("nb", [P, 1], F32, 4)
-            nc.scalar.mul(s[:], state["mx", n][:], -INV)
-            state["nb", n] = s
+        def s2_shift(n):
+            live["shift", n] = work("row_shift", [P, 1], F32, 4)
+            nc.scalar.mul(live["shift", n][:], live["max", n][:], -INV_SQRT_D)
 
-        def exps(n):
-            e = sb("e", [P, M], F32, 3)
-            s = sb("sum", [P, 1], F32, 4)
+        def s2_exp(n):
+            live["exp", n] = work("row_exp", [P, M], F32, 4)
+            live["sum", n] = work("row_sum", [P, 1], F32, 4)
             nc.scalar.activation(
-                e[:], state["s2", n][:], ACT.Exp, bias=state["nb", n][:], scale=INV, accum_out=s[:]
+                live["exp", n][:],
+                live["s2", n][:],
+                ACT.Exp,
+                bias=live["shift", n][:],
+                scale=INV_SQRT_D,
+                accum_out=live["sum", n][:],
             )
-            state["e", n] = (e, s)
 
-        def recip(n):
-            r = sb("rs", [P, 1], F32, 4)
-            nc.vector.reciprocal(out=r[:], in_=state["e", n][1][:])
-            state["rs", n] = r
+        def p2_reciprocal(n):
+            live["1/sum", n] = work("row_inverse", [P, 1], F32, 4)
+            nc.vector.reciprocal(out=live["1/sum", n][:], in_=live["sum", n][:])
 
-        def norm(n):
+        def p2_scale(n):
             k, j = divmod(n, 2)
-            e, r = state["e", n][0], state["rs", n]
             if j == 0:
-                state["p2", k] = sb("p2", [P, 2, M], BF16, 3)
+                live["p2", k] = work("p2_rows", [P, 2, M], BF16, 3)
             nc.vector.scalar_tensor_tensor(
-                out=state["p2", k][:, j, :], in0=e[:], scalar=r[:], in1=g2b[:], op0=ALU.mult, op1=ALU.mult
+                out=live["p2", k][:, j, :],
+                in0=live["exp", n][:],
+                scalar=live["1/sum", n][:],
+                in1=g2_all[:],
+                op0=ALU.mult,
+                op1=ALU.mult,
             )
 
-        def tr_p(k):
-            words = state["p2", k][:].rearrange("p j m -> p (j m)").bitcast(F32)
-            x = ps("b", [P, 2, 2, P], F32, NBANK)
+        def p2_turn(k):
+            words = live["p2", k][:].rearrange("p j m -> p (j m)").bitcast(F32)
+            x = bank([P, 2, 2, P], F32)
             for j in range(2):
                 for u in range(2):
                     lo = (2 * j + u) * P
                     nc.tensor.transpose(x[:, j, u, :], words[:, lo : lo + P], ident[:])
-            state["trp", k] = x
+            live["p2 turned", k] = x
 
-        def cp_p(k):
-            g = sb("p2g", [P, 2, P, 4], BF16, 2)
-            nc.scalar.copy(out=words4(g), in_=state["trp", k][:].rearrange("p j u r -> p j r u"))
-            state["p2g", k] = g
+        def p2_copy(k):
+            g = work("p2_grouped", [P, 2, P, PACK], BF16, 2)
+            nc.scalar.copy(out=word_pairs(g[:]), in_=live["p2 turned", k][:].rearrange("p j u r -> p j r u"))
+            live["p2 grouped", k] = g
 
-        def qz_p(k):
-            c = sb("p2c", [P, 2 * P], U32, 2 + DELTA)
-            s = sb("p2s", [P, 2 * P], U8, 2 + DELTA)
-            quant(c[:], s[:], state["p2g", k][:].rearrange("p j r t -> p (j r t)"))
-            state["p2c", k] = (c, s)
+        def p2_quantize(k):
+            live["p2 mx", k] = mx_pair("p2", [P, 2 * P], OUT_LAG)
+            quantize(live["p2 mx", k], (ALL, ALL), live["p2 grouped", k][:].rearrange("p j r t -> p (j r t)"))
 
-        def mm_3(k):
-            b = k // PAIRS
-            xs = []
+        def out_multiply(k):
             for j in range(2):
-                x = ps("b", [P, D], F32, NBANK)
-                mx(x[:], state["p2c", k], state["uc", b], (ALL, slice(j * P, (j + 1) * P)), (ALL, ALL))
-                xs.append(x)
-            state["ox", k] = xs
+                x = bank([P, D], F32)
+                multiply(x[:], live["p2 mx", k], (ALL, slice(j * P, (j + 1) * P)), live["u mx", k // PAIRS], (ALL, ALL))
+                live["out bank", k, j] = x
 
-        def out_copy(k, j, eng):
+        def out_copy(k, j, copy):
             if j == 0:
-                state["o", k] = sb("o_sb", [P, 2, D], F32, 4)
-            eng(out=state["o", k][:, j, :], in_=state["ox", k][j][:])
+                live["out", k] = work("out_rows", [P, 2, D], F32, 4)
+            copy(out=live["out", k][:, j, :], in_=live["out bank", k, j][:])
 
-        def store(k):
+        def out_store(k, tiles):
             b, i = divmod(k, PAIRS)
-            nc.sync.dma_start(
-                out=out[b].rearrange("(p j) d -> p j d", j=8)[:, 2 * i : 2 * i + 2, :], in_=state["o", k][:]
-            )
+            for lo, hi in tiles:
+                nc.sync.dma_start(out=out_dst[b][:, 2 * i + lo : 2 * i + hi, :], in_=live["out", k][:, lo:hi, :])
 
-        f1 = sb("f1", [P, 4, 512], BF16, 1)
-        f2 = sb("f2", [P, 4, 256], BF16, 1)
-        f3 = sb("f3", [P, 4, 128], BF16, 1)
-        nm1 = keep("nm1", [P, 4], F32)
-        mx1 = keep("mx1", [P, 4], F32)
-        sum1 = keep("sum1", [P, 4], F32)
-        r1 = keep("r1", [P, 4], F32)
-        p1c = (keep("p1c", [P, 4, 2, P], U32), keep("p1s", [P, 4, 2, P], U8))
-        state["p1c"] = p1c
+        widths = (N // 2, N // 4, N // 8)
+        folded = [work("fold_%d" % w, [P, M // P, w], BF16, 1) for w in widths]
+        p1_max = keep("p1_max", [P, M // P], F32)
+        p1_shift = keep("p1_shift", [P, M // P], F32)
+        p1_sum = keep("p1_sum", [P, M // P], F32)
+        p1_inverse = keep("p1_inverse", [P, M // P], F32)
+        p1_mx = (keep("p1_codes", [P, M // P, 2, P], U32), keep("p1_scales", [P, M // P, 2, P], U8))
 
         def p1_fold(h, i):
-            hs = slice(2 * h, 2 * h + 2)
-            src, dst, w = ((b1_sb, f1, 512), (f1, f2, 256), (f2, f3, 128))[i]
-            nc.vector.tensor_tensor(out=dst[:, hs, :], in0=src[:, hs, 0:w], in1=src[:, hs, w : 2 * w], op=ALU.max)
+            rows = slice(2 * h, 2 * h + 2)
+            src = folded[i - 1] if i else b1_rows
+            w = widths[i]
+            nc.vector.tensor_tensor(
+                out=folded[i][:, rows, :], in0=src[:, rows, 0:w], in1=src[:, rows, w : 2 * w], op=ALU.max
+            )
 
-        def p1_max(h):
-            hs = slice(2 * h, 2 * h + 2)
-            nc.vector.tensor_reduce(out=mx1[:, hs], in_=f3[:, hs, :], axis=AX.X, op=ALU.max)
-            nc.scalar.mul(nm1[:, hs], mx1[:, hs], -1.0)
+        def p1_reduce(h):
+            rows = slice(2 * h, 2 * h + 2)
+            nc.vector.tensor_reduce(out=p1_max[:, rows], in_=folded[2][:, rows, :], axis=AX.X, op=ALU.max)
+
+        def p1_negate(h):
+            rows = slice(2 * h, 2 * h + 2)
+            nc.scalar.mul(p1_shift[:, rows], p1_max[:, rows], -1.0)
 
         def p1_exp(t):
-            e1 = sb("e1", [P, N], F32, 2)
-            nc.scalar.activation(e1[:], b1_sb[:, t, :], ACT.Exp, bias=nm1[:, t : t + 1], accum_out=sum1[:, t : t + 1])
-            state["e1", t] = e1
-
-        def p1_recip(t):
-            nc.vector.reciprocal(out=r1[:, t : t + 1], in_=sum1[:, t : t + 1])
-
-        def p1_norm(t):
-            p1 = sb("p1", [P, N], BF16, 2)
-            nc.vector.scalar_tensor_tensor(
-                out=p1[:], in0=state["e1", t][:], scalar=r1[:, t : t + 1], in1=g1b[:], op0=ALU.mult, op1=ALU.mult
+            col = slice(t, t + 1)
+            live["p1 exp", t] = work("p1_exp", [P, N], F32, 2)
+            nc.scalar.activation(
+                live["p1 exp", t][:], b1_rows[:, t, :], ACT.Exp, bias=p1_shift[:, col], accum_out=p1_sum[:, col]
             )
-            state["p1", t] = p1
 
-        def p1_tr(t):
-            words = state["p1", t][:].bitcast(F32)
-            x = ps("b", [P, 2, 2, P], F32, NBANK)
+        def p1_reciprocal(t):
+            col = slice(t, t + 1)
+            nc.vector.reciprocal(out=p1_inverse[:, col], in_=p1_sum[:, col])
+
+        def p1_scale(t):
+            live["p1", t] = work("p1_rows", [P, N], BF16, 2)
+            nc.vector.scalar_tensor_tensor(
+                out=live["p1", t][:],
+                in0=live["p1 exp", t][:],
+                scalar=p1_inverse[:, t : t + 1],
+                in1=g1_all[:],
+                op0=ALU.mult,
+                op1=ALU.mult,
+            )
+
+        def p1_turn(t):
+            words = live["p1", t][:].bitcast(F32)
+            x = bank([P, 2, 2, P], F32)
             for g in range(2):
                 for u in range(2):
                     nc.tensor.transpose(x[:, g, u, :], words[:, 256 * g + u : 256 * (g + 1) : 2], ident[:])
-            state["p1x", t] = x
+            live["p1 turned", t] = x
 
-        def p1_cp(t):
-            pg = sb("p1g", [P, 2, P, 4], BF16, 2)
-            nc.scalar.copy(out=words4(pg), in_=state["p1x", t][:].rearrange("p g u r -> p g r u"))
-            state["p1g", t] = pg
+        def p1_copy(t):
+            g = work("p1_grouped", [P, 2, P, PACK], BF16, 2)
+            nc.scalar.copy(out=word_pairs(g[:]), in_=live["p1 turned", t][:].rearrange("p g u r -> p g r u"))
+            live["p1 grouped", t] = g
 
-        def p1_qz(t):
-            quant(
-                p1c[0][:, t].rearrange("p g m -> p (g m)"),
-                p1c[1][:, t].rearrange("p g m -> p (g m)"),
-                state["p1g", t][:].rearrange("p g r t -> p (g r t)"),
+        def p1_quantize(t):
+            nc.vector.quantize_mx(
+                out=p1_mx[0][:, t].rearrange("p g m -> p (g m)").bitcast(X4),
+                scales=p1_mx[1][:, t].rearrange("p g m -> p (g m)"),
+                in_=live["p1 grouped", t][:].rearrange("p g r t -> p (g r t)"),
             )
 
+        def chunk_of(k):
+            n = k + 3 - V_LAG
+            return divmod(n, CHUNKS) if 0 <= n < B * CHUNKS else None
 
-        def v_unit(s):
-            n = s + 3 - DELTA
-            return divmod(n, PAIRS) if 0 <= n < B * PAIRS else None
-
-        def w_unit(s, engs):
-            n = s + 8 - DELTA
+        def widen_step(k, engine):
+            n = k + 8 - V_LAG
             if 0 <= n < B * PAIRS:
                 b, i = divmod(n, PAIRS)
-                for w in range(2):
-                    if engs[w] != "-":
-                        widen(b, 2 * i + w, engs[w])
+                for w in (2 * i, 2 * i + 1):
+                    on = "scalar" if w % 4 == 0 else "vector"
+                    if on == engine:
+                        v_widen(b, w, engine)
 
         for i in range(3):
             p1_fold(0, i)
-        p1_max(0)
-        tr_a(0, 0)
-        cp_a(0, 0, nc.scalar.copy)
-        tr_a(0, 1)
-        cp_a(0, 1, nc.vector.tensor_copy)
-        tr_q(0)
-        cp_q(0)
+        p1_reduce(0)
+        p1_negate(0)
+        a_turn(0, 0)
+        a_turn(0, 1)
+        q_turn(0)
+        a_copy(0, 0, nc.scalar.copy)
+        a_copy(0, 1, nc.vector.tensor_copy)
+        q_copy(0)
         p1_exp(0)
-        qz_a(0)
         p1_fold(1, 0)
-        qz_q(0)
-        mm_2(0)
-        mm_2(1)
+        a_quantize(0)
         p1_fold(1, 1)
+        v_widen(0, 7, "scalar")
+        v_widen(0, 5, "scalar")
+        v_widen(0, 2, "vector")
+        q_quantize(0)
+        v_widen(0, 0, "vector")
         p1_exp(1)
-        p1_recip(0)
         p1_fold(1, 2)
-        maxes(0)
-        p1_max(1)
-        p1_norm(0)
-        shift(0)
-        tr_q(1)
-        cp_q(1)
-        p1_tr(0)
-        exps(0)
-        nc.scalar.copy(
-            out=g2b[:].rearrange("p (u h e) -> p u h e", u=2, e=2),
-            in_=g2n[:].rearrange("p (h u e) -> p u h e", u=2, e=2),
-        )
-        p1_recip(1)
+        p1_reciprocal(0)
+        p1_reduce(1)
+        p1_negate(1)
+        p1_scale(0)
+        v_widen(0, 1, "scalar")
+        p1_reciprocal(1)
         p1_exp(2)
-        widen(0, 0, "v")
-        p1_cp(0)
-        p1_norm(1)
-        p1_tr(1)
+        p1_turn(0)
+        s2_multiply(0)
+        widen_step(-1, "vector")
+        p1_copy(0)
+        p1_scale(1)
+        p1_turn(1)
+        q_turn(1)
+        s2_multiply(1)
         p1_exp(3)
-        widen(0, 1, "s")
-        p1_recip(2)
-        widen(0, 2, "v")
-        p1_norm(2)
-        widen(0, 3, "s")
-        p1_cp(1)
-        widen(0, 4, "v")
-        p1_recip(3)
-        p1_qz(0)
-        p1_tr(2)
-        p1_norm(3)
-        widen(0, 5, "s")
-        widen(0, 6, "v")
-        p1_cp(2)
-        widen(0, 7, "s")
-        p1_qz(1)
-        mm_v(0, 0)
-        p1_tr(3)
-        mm_v(0, 1)
-        p1_qz(2)
-        cp_v(0, 0)
-        p1_cp(3)
-        cp_v(0, 1)
-        w_unit(DELTA - 4, "vv")
-        qz_v(0, 0)
-        p1_qz(3)
-        mm_1(0, 0)
-        w_unit(DELTA - 3, "vs")
-        tt_u(0, 0)
+        v_widen(0, 3, "scalar")
+        p1_reciprocal(2)
+        v_widen(0, 6, "vector")
+        p1_scale(2)
+        p1_copy(1)
+        q_copy(1)
+        p1_turn(2)
+        p1_quantize(0)
+        p1_reciprocal(3)
+        v_widen(0, 4, "vector")
+        v_interleave(0, 0)
+        p1_scale(3)
+        p1_copy(2)
+        p1_turn(3)
+        v_interleave(0, 1)
+        widen_step(-2, "vector")
+        p1_quantize(1)
+        v_copy(0, 0)
+        s2_max(0)
+        p1_copy(3)
+        v_quantize(0, 0)
+        s2_shift(0)
+        s2_exp(0)
+        p1_quantize(2)
+        p1_quantize(3)
+        widen_step(-2, "scalar")
+        v_copy(0, 1)
+        nc.scalar.copy(
+            out=g2_all[:].rearrange("p (u h e) -> p u h e", u=2, e=2),
+            in_=g2_plain[:].rearrange("p (h u e) -> p u h e", u=2, e=2),
+        )
+        t_multiply(0, 0)
 
-        for k in range(STEPS + L3):
+        for k in range(STEPS + OUT_LAG):
             b, i = divmod(k, PAIRS)
-            main = k < STEPS
+            chunk, chunk_before, chunk_after = chunk_of(k), chunk_of(k - 1), chunk_of(k + 1)
+            a_half = (b + 1, i - 1) if i in (1, 2) and b + 1 < B else None
+            ready = k - OUT_LAG
             if i == 0 and b + 2 < B:
                 load_a(b + 2)
-                load_q(b + 2, [(0, 4), (4, 8)])
+                load_q(b + 2, 0)
+                load_q(b + 2, 1)
                 load_v(b + 2)
-            unit = v_unit(k)
-            after = v_unit(k + 1)
-            before = v_unit(k - 1)
-            q_next = k + 2 if k + 2 < STEPS else None
-            a_half = (b + 1, i - 1) if i in (1, 2) and b + 1 < B else None
-            done = k - L3 if k >= L3 else None
-            late = k >= STEPS
+            if k < STEPS:
+                s2_max(2 * k + 1)
             if 1 <= k <= STEPS:
-                tr_p(k - 1)
-            if q_next:
-                tr_q(q_next)
+                p2_scale(2 * k - 1)
+            if i == 3 and b + 1 < B:
+                a_quantize(b + 1)
             if a_half:
-                tr_a(*a_half)
-            if main:
-                maxes(2 * k + 1)
+                a_turn(*a_half)
             if 1 <= k <= STEPS:
-                cp_p(k - 1)
-            if main:
-                shift(2 * k + 1)
-            if unit and k >= 1 - (DELTA < 3) * 0 and ("vg", *unit) not in state:
-                cp_v(*unit)
-            if main:
-                recip(2 * k)
-            if k + 1 < STEPS:
-                qz_q(k + 1)
-                mm_2(2 * k + 2)
-                mm_2(2 * k + 3)
-            if before:
-                qz_u(*before)
-            if main:
-                norm(2 * k)
-                exps(2 * k + 1)
-            if q_next:
-                cp_q(q_next)
-            if 1 <= k <= STEPS:
-                qz_p(k - 1)
-            if unit and ("vc", *unit) not in state:
-                qz_v(*unit)
-            if done is not None:
-                mm_3(done)
-            if unit:
-                mm_1(*unit)
-            if after and ("vx", *after) not in state:
-                mm_v(*after)
+                p2_turn(k - 1)
+            if k + 2 < STEPS:
+                q_turn(k + 2)
+            if 1 <= k < STEPS:
+                s2_exp(2 * k)
+            if k < STEPS:
+                s2_shift(2 * k + 1)
+            if chunk and k >= 1:
+                v_copy(*chunk)
+            if k < STEPS:
+                s2_exp(2 * k + 1)
             if a_half:
-                cp_a(*a_half, nc.scalar.copy)
-            w_unit(k, ENGS[k % 4].replace("v", "-"))
+                a_copy(*a_half, nc.scalar.copy)
+            widen_step(k, "scalar")
+            if 1 <= k <= STEPS:
+                p2_copy(k - 1)
+            if k + 2 < STEPS:
+                q_copy(k + 2)
+            if chunk_before:
+                u_scale(*chunk_before)
             if k + 1 < STEPS:
-                maxes(2 * k + 2)
-                shift(2 * k + 2)
-            if done is not None:
-                out_copy(done, 0, nc.scalar.copy)
-            if main:
-                recip(2 * k + 1)
-            w_unit(k, ENGS[k % 4].replace("s", "-"))
-            if main:
-                norm(2 * k + 1)
+                q_quantize(k + 1)
+            if k >= 1:
+                widen_step(k - 1, "vector")
+            if 2 <= k <= STEPS + 1:
+                p2_quantize(k - 2)
+            if k < STEPS:
+                p2_reciprocal(2 * k)
+            if chunk_before:
+                u_quantize(*chunk_before)
+            if chunk:
+                v_quantize(*chunk)
+            if k < STEPS:
+                p2_scale(2 * k)
             if k + 1 < STEPS:
-                exps(2 * k + 2)
-            if done is not None:
-                out_copy(done, 1, nc.vector.tensor_copy if late else nc.scalar.copy)
-                store(done)
-            if unit:
-                tt_u(*unit)
-            if i == 2 and b + 1 < B:
-                qz_a(b + 1)
+                s2_multiply(2 * k + 2)
+                s2_multiply(2 * k + 3)
+                s2_max(2 * k + 2)
+            if k < STEPS:
+                p2_reciprocal(2 * k + 1)
+            if ready >= 0:
+                out_multiply(ready)
+            if chunk:
+                t_multiply(*chunk)
+            if chunk_after:
+                v_interleave(*chunk_after)
+            if ready >= 0:
+                out_copy(ready, 0, nc.scalar.copy)
+            if k + 1 < STEPS:
+                s2_shift(2 * k + 2)
+            if ready >= 0:
+                if k < STEPS:
+                    out_copy(ready, 1, nc.scalar.copy)
+                    out_store(ready, [(0, 2)])
+                else:
+                    out_copy(ready, 1, nc.vector.tensor_copy)
+                    out_store(ready, [(0, 1), (1, 2)])

from contextlib import ExitStack

import concourse.mybir as mybir
from concourse.masks import make_identity

B, N, M, D = 6, 1024, 512, 512
FLOPS = 3 * 2 * B * N * M * D

F32 = mybir.dt.float32
BF16 = mybir.dt.bfloat16
U32 = mybir.dt.uint32
U8 = mybir.dt.uint8
FP8 = mybir.dt.float8_e4m3fn
X4 = mybir.dt.float8_e4m3fn_x4
ALU = mybir.AluOpType
ACT = mybir.ActivationFunctionType
AX = mybir.AxisListType

P = 128
PACK = 4
INV_SQRT_D = 1.0 / (D**0.5)
TILES = N // P
PAIRS = TILES // 2
STEPS = B * PAIRS
CHUNKS = D // P
BANKS = 5
S2_BANKS = 3
V_LAG = 2
OUT_LAG = 1 + V_LAG


def tile_agentattentionbiased_t_kernel(tc, q, a, v_bytes, v_scale, b1, g1, g2, g3, out):
    nc = tc.nc
    with ExitStack() as ctx:
        const = ctx.enter_context(tc.tile_pool(name="const", bufs=1))
        pool = ctx.enter_context(tc.tile_pool(name="work", bufs=2))
        psum = ctx.enter_context(tc.psum_pool(name="psum", bufs=2))
        ctx.enter_context(tc.manual_schedule())

        def keep(tag, shape, dtype):
            return const.tile(shape, dtype, name=tag, tag=tag, align_bytes=64)

        def work(tag, shape, dtype, bufs):
            return pool.tile(shape, dtype, name=tag, tag=tag, bufs=bufs, align_bytes=64)

        def bank(shape, dtype):
            return psum.tile(shape, dtype, name="bank", tag="bank", bufs=BANKS)

        def mx_pair(tag, shape, bufs):
            return work(tag + "_codes", shape, U32, bufs), work(tag + "_scales", shape, U8, bufs)

        def quantize(dst, cols, src):
            nc.vector.quantize_mx(out=dst[0][cols].bitcast(X4), scales=dst[1][cols], in_=src)

        def multiply(dst, left, left_cols, right, right_cols, start=True, stop=True):
            nc.tensor.matmul_mx(
                dst,
                lhsT=left[0][left_cols].bitcast(X4),
                lhsT_scale=left[1][left_cols],
                rhs=right[0][right_cols].bitcast(X4),
                rhs_scale=right[1][right_cols],
                start=start,
                stop=stop,
            )

        def word_pairs(t):
            return t.rearrange("p j r t -> p (j r t)").bitcast(F32).rearrange("p (j r u) -> p j r u", j=2, u=2)

        ALL = slice(None)
        live = {}

        q_src = [q[b].rearrange("(p j) d -> p j d", j=TILES) for b in range(B)]
        out_dst = [out[b].rearrange("(p j) d -> p j d", j=TILES) for b in range(B)]

        def load_a(b):
            live["a", b] = work("a_rows", [P, M // P, D], BF16, 2)
            nc.sync.dma_start(out=live["a", b][:], in_=a[b].rearrange("(j p) d -> p j d", p=P))

        def load_q(b, half):
            if half == 0:
                live["q", b] = work("q_rows", [P, TILES, D], BF16, 3)
            tiles = slice(half * TILES // 2, (half + 1) * TILES // 2)
            nc.sync.dma_start(out=live["q", b][:, tiles, :], in_=q_src[b][:, tiles, :])

        def load_v(b):
            live["v bytes", b] = work("v_raw", [P, 2, PACK, D], U8, 3)
            nc.sync.dma_start(
                out=live["v bytes", b][:].rearrange("p g t d -> p g (t d)"),
                in_=v_bytes[b].rearrange("(g p t) d -> p g (t d)", g=2, t=PACK),
            )

        one = keep("one", [P, 1], F32)
        nc.vector.memset(one[:], 0.0)
        one_exp = keep("one_exp", [P, 1], F32)
        nc.scalar.activation(one_exp[:], one[:], ACT.Exp)

        b1_rows = keep("b1_rows", [P, M // P, N], BF16)
        b1_src = b1.rearrange("(m t) n -> m t n", t=PACK)
        nc.sync.dma_start(out=b1_rows[:, 0:2, :], in_=b1_src[:, 0:2, :])
        load_a(0)
        load_q(0, 0)
        nc.sync.dma_start(out=b1_rows[:, 2:4, :], in_=b1_src[:, 2:4, :])
        v_factor = keep("v_factor", [P, 2, PACK], F32)
        nc.scalar.dma_start(out=v_factor[:], in_=v_scale.rearrange("o (g p t) x -> p (o g) (t x)", g=2, t=PACK))
        g3_cols = keep("g3_cols", [P, PACK], BF16)
        nc.scalar.dma_start(out=g3_cols[:], in_=g3.rearrange("(p t) -> p t", t=PACK))
        g2_plain = keep("g2_plain", [P, M], BF16)
        nc.sync.dma_start(out=g2_plain[:], in_=g2.partition_broadcast(P))
        load_v(0)
        g1_all = keep("g1_all", [P, N], BF16)
        nc.sync.dma_start(out=g1_all[:], in_=g1.partition_broadcast(P))
        load_q(0, 1)
        load_v(1)
        load_a(1)
        load_q(1, 0)
        load_q(1, 1)

        ident = keep("ident", [P, P], F32)
        make_identity(nc, ident[:])
        perm = keep("perm", [P, P], F32)
        nc.gpsimd.tensor_copy(
            out=perm[:].rearrange("p (u h e) -> p u h e", u=2, e=2),
            in_=ident[:].rearrange("p (h u e) -> p u h e", u=2, e=2),
        )
        ident16 = keep("ident16", [P, P], BF16)
        nc.gpsimd.tensor_copy(out=ident16[:], in_=ident[:])
        g2_all = keep("g2_all", [P, M], BF16)

        def turn(rows, first, identity):
            words = rows[:].rearrange("p j d -> p (j d)").bitcast(F32)
            x = bank([P, 2, 2, P], F32)
            for j in range(2):
                lo = (first + j) * (D // 2)
                for u in range(2):
                    nc.tensor.transpose(x[:, j, u, :], words[:, lo + u : lo + D // 2 : 2], identity[:])
            return x

        def q_turn(k):
            b, i = divmod(k, PAIRS)
            live["q turned", k] = turn(live["q", b], 2 * i, ident)

        def q_copy(k):
            g = work("q_grouped", [P, 2, P, PACK], BF16, 3)
            nc.scalar.copy(out=word_pairs(g[:]), in_=live["q turned", k][:].rearrange("p j u r -> p j r u"))
            live["q grouped", k] = g

        def q_quantize(k):
            live["q mx", k] = mx_pair("q", [P, 2 * P], 3)
            quantize(live["q mx", k], (ALL, ALL), live["q grouped", k][:].rearrange("p j r t -> p (j r t)"))

        def a_turn(b, h):
            live["a turned", b, h] = turn(live["a", b], 2 * h, perm)

        def a_copy(b, h, copy):
            if h == 0:
                live["a grouped", b] = work("a_grouped", [P, 2, 2, P, PACK], BF16, 2)
            dst = live["a grouped", b][:].rearrange("p u h r t -> p (u h r t)").bitcast(F32)
            dst = dst.rearrange("p (u h j r w) -> p u h j r w", u=2, h=2, j=2, w=2)
            src = live["a turned", b, h][:].rearrange("p j w (u r) -> p u j r w", u=2)
            for u in range(2):
                copy(out=dst[:, u, h], in_=src[:, u])

        def a_quantize(b):
            live["a mx", b] = mx_pair("a", [P, M], 2)
            quantize(live["a mx", b], (ALL, ALL), live["a grouped", b][:].rearrange("p u h r t -> p (u h r t)"))

        def v_widen(b, w, engine):
            if ("v wide", b) not in live:
                live["v wide", b] = work("v_wide", [P, 2, PACK, D], BF16, 2)
            g, t = divmod(w, PACK)
            src = live["v bytes", b][:, g, t, :].bitcast(FP8)
            dst = live["v wide", b][:, g, t, :]
            factor = v_factor[:, g, t : t + 1]
            if engine == "vector":
                nc.vector.tensor_scalar(out=dst, in0=src, scalar1=factor, scalar2=None, op0=ALU.mult)
            else:
                nc.scalar.activation(dst, src, ACT.Copy, scale=factor)

        def v_interleave(b, c):
            x = bank([P, 2, P, PACK], BF16)
            for g in range(2):
                nc.tensor.matmul(
                    x[:, g].rearrange("p d t -> p t d"),
                    lhsT=ident16[:],
                    rhs=live["v wide", b][:, g, :, c * P : (c + 1) * P],
                    start=True,
                    stop=True,
                )
            live["v bank", b, c] = x

        def v_copy(b, c):
            g = work("v_grouped", [P, 2, P, PACK], BF16, 3)
            nc.scalar.copy(
                out=g[:].rearrange("p g d t -> p (g d t)"),
                in_=live["v bank", b, c][:].rearrange("p g d t -> p (g d t)"),
            )
            live["v grouped", b, c] = g

        def v_quantize(b, c):
            live["v mx", b, c] = mx_pair("v", [P, 2 * P], 4)
            quantize(live["v mx", b, c], (ALL, ALL), live["v grouped", b, c][:].rearrange("p g d t -> p (g d t)"))

        def t_multiply(b, c):
            x = bank([P, PACK, P], F32)
            for t in range(PACK):
                for g in range(2):
                    multiply(
                        x[:, t, :], p1_mx, (ALL, t, g, ALL), live["v mx", b, c], (ALL, slice(g * P, (g + 1) * P)), g == 0, g == 1
                    )
            live["t bank", b, c] = x

        def u_scale(b, c):
            g = work("u_grouped", [P, P, PACK], BF16, 2)
            nc.vector.tensor_tensor(
                out=g[:],
                in0=live["t bank", b, c][:].rearrange("p t d -> p d t"),
                in1=g3_cols[:].unsqueeze(1).to_broadcast([P, P, PACK]),
                op=ALU.mult,
            )
            live["u grouped", b, c] = g

        def u_quantize(b, c):
            if c == 0:
                live["u mx", b] = mx_pair("u", [P, D], 3)
            quantize(live["u mx", b], (ALL, slice(c * P, (c + 1) * P)), live["u grouped", b, c][:].rearrange("p d t -> p (d t)"))

        def s2_multiply(n):
            k, j = divmod(n, 2)
            x = psum.tile([P, M], F32, name="s2", tag="s2", bufs=S2_BANKS)
            multiply(x[:], live["q mx", k], (ALL, slice(j * P, (j + 1) * P)), live["a mx", k // PAIRS], (ALL, ALL))
            live["s2", n] = x

        def s2_max(n):
            live["max", n] = work("row_max", [P, 1], F32, 4)
            nc.vector.tensor_reduce(out=live["max", n][:], in_=live["s2", n][:], axis=AX.X, op=ALU.max)

        def s2_shift(n):
            live["shift", n] = work("row_shift", [P, 1], F32, 4)
            nc.scalar.mul(live["shift", n][:], live["max", n][:], -INV_SQRT_D)

        def s2_exp(n):
            live["exp", n] = work("row_exp", [P, M], F32, 4)
            live["sum", n] = work("row_sum", [P, 1], F32, 4)
            nc.scalar.activation(
                live["exp", n][:],
                live["s2", n][:],
                ACT.Exp,
                bias=live["shift", n][:],
                scale=INV_SQRT_D,
                accum_out=live["sum", n][:],
            )

        def p2_reciprocal(n):
            live["1/sum", n] = work("row_inverse", [P, 1], F32, 4)
            nc.vector.reciprocal(out=live["1/sum", n][:], in_=live["sum", n][:])

        def p2_scale(n):
            k, j = divmod(n, 2)
            if j == 0:
                live["p2", k] = work("p2_rows", [P, 2, M], BF16, 3)
            nc.vector.scalar_tensor_tensor(
                out=live["p2", k][:, j, :],
                in0=live["exp", n][:],
                scalar=live["1/sum", n][:],
                in1=g2_all[:],
                op0=ALU.mult,
                op1=ALU.mult,
            )

        def p2_turn(k):
            words = live["p2", k][:].rearrange("p j m -> p (j m)").bitcast(F32)
            x = bank([P, 2, 2, P], F32)
            for j in range(2):
                for u in range(2):
                    lo = (2 * j + u) * P
                    nc.tensor.transpose(x[:, j, u, :], words[:, lo : lo + P], ident[:])
            live["p2 turned", k] = x

        def p2_copy(k):
            g = work("p2_grouped", [P, 2, P, PACK], BF16, 2)
            nc.scalar.copy(out=word_pairs(g[:]), in_=live["p2 turned", k][:].rearrange("p j u r -> p j r u"))
            live["p2 grouped", k] = g

        def p2_quantize(k):
            live["p2 mx", k] = mx_pair("p2", [P, 2 * P], OUT_LAG)
            quantize(live["p2 mx", k], (ALL, ALL), live["p2 grouped", k][:].rearrange("p j r t -> p (j r t)"))

        def out_multiply(k):
            for j in range(2):
                x = bank([P, D], F32)
                multiply(x[:], live["p2 mx", k], (ALL, slice(j * P, (j + 1) * P)), live["u mx", k // PAIRS], (ALL, ALL))
                live["out bank", k, j] = x

        def out_copy(k, j, copy):
            if j == 0:
                live["out", k] = work("out_rows", [P, 2, D], F32, 4)
            copy(out=live["out", k][:, j, :], in_=live["out bank", k, j][:])

        def out_store(k, tiles):
            b, i = divmod(k, PAIRS)
            for lo, hi in tiles:
                nc.sync.dma_start(out=out_dst[b][:, 2 * i + lo : 2 * i + hi, :], in_=live["out", k][:, lo:hi, :])

        widths = (N // 2, N // 4, N // 8)
        folded = [work("fold_%d" % w, [P, M // P, w], BF16, 1) for w in widths]
        p1_max = keep("p1_max", [P, M // P], F32)
        p1_shift = keep("p1_shift", [P, M // P], F32)
        p1_sum = keep("p1_sum", [P, M // P], F32)
        p1_inverse = keep("p1_inverse", [P, M // P], F32)
        p1_mx = (keep("p1_codes", [P, M // P, 2, P], U32), keep("p1_scales", [P, M // P, 2, P], U8))

        def p1_fold(h, i):
            rows = slice(2 * h, 2 * h + 2)
            src = folded[i - 1] if i else b1_rows
            w = widths[i]
            nc.vector.tensor_tensor(
                out=folded[i][:, rows, :], in0=src[:, rows, 0:w], in1=src[:, rows, w : 2 * w], op=ALU.max
            )

        def p1_reduce(h):
            rows = slice(2 * h, 2 * h + 2)
            nc.vector.tensor_reduce(out=p1_max[:, rows], in_=folded[2][:, rows, :], axis=AX.X, op=ALU.max)

        def p1_negate(h):
            rows = slice(2 * h, 2 * h + 2)
            nc.scalar.mul(p1_shift[:, rows], p1_max[:, rows], -1.0)

        def p1_exp(t):
            col = slice(t, t + 1)
            live["p1 exp", t] = work("p1_exp", [P, N], F32, 2)
            nc.scalar.activation(
                live["p1 exp", t][:], b1_rows[:, t, :], ACT.Exp, bias=p1_shift[:, col], accum_out=p1_sum[:, col]
            )

        def p1_reciprocal(t):
            col = slice(t, t + 1)
            nc.vector.reciprocal(out=p1_inverse[:, col], in_=p1_sum[:, col])

        def p1_scale(t):
            live["p1", t] = work("p1_rows", [P, N], BF16, 2)
            nc.vector.scalar_tensor_tensor(
                out=live["p1", t][:],
                in0=live["p1 exp", t][:],
                scalar=p1_inverse[:, t : t + 1],
                in1=g1_all[:],
                op0=ALU.mult,
                op1=ALU.mult,
            )

        def p1_turn(t):
            words = live["p1", t][:].bitcast(F32)
            x = bank([P, 2, 2, P], F32)
            for g in range(2):
                for u in range(2):
                    nc.tensor.transpose(x[:, g, u, :], words[:, 256 * g + u : 256 * (g + 1) : 2], ident[:])
            live["p1 turned", t] = x

        def p1_copy(t):
            g = work("p1_grouped", [P, 2, P, PACK], BF16, 2)
            nc.scalar.copy(out=word_pairs(g[:]), in_=live["p1 turned", t][:].rearrange("p g u r -> p g r u"))
            live["p1 grouped", t] = g

        def p1_quantize(t):
            nc.vector.quantize_mx(
                out=p1_mx[0][:, t].rearrange("p g m -> p (g m)").bitcast(X4),
                scales=p1_mx[1][:, t].rearrange("p g m -> p (g m)"),
                in_=live["p1 grouped", t][:].rearrange("p g r t -> p (g r t)"),
            )

        def chunk_of(k):
            n = k + 3 - V_LAG
            return divmod(n, CHUNKS) if 0 <= n < B * CHUNKS else None

        def widen_step(k, engine):
            n = k + 8 - V_LAG
            if 0 <= n < B * PAIRS:
                b, i = divmod(n, PAIRS)
                for w in (2 * i, 2 * i + 1):
                    on = "scalar" if w % 4 == 0 else "vector"
                    if on == engine:
                        v_widen(b, w, engine)

        for i in range(3):
            p1_fold(0, i)
        p1_reduce(0)
        p1_negate(0)
        a_turn(0, 0)
        a_turn(0, 1)
        q_turn(0)
        a_copy(0, 0, nc.scalar.copy)
        a_copy(0, 1, nc.vector.tensor_copy)
        q_copy(0)
        p1_exp(0)
        p1_fold(1, 0)
        a_quantize(0)
        p1_fold(1, 1)
        v_widen(0, 7, "scalar")
        v_widen(0, 5, "scalar")
        v_widen(0, 2, "vector")
        q_quantize(0)
        v_widen(0, 0, "vector")
        p1_exp(1)
        p1_fold(1, 2)
        p1_reciprocal(0)
        p1_reduce(1)
        p1_negate(1)
        p1_scale(0)
        v_widen(0, 1, "scalar")
        p1_reciprocal(1)
        p1_exp(2)
        p1_turn(0)
        s2_multiply(0)
        widen_step(-1, "vector")
        p1_copy(0)
        p1_scale(1)
        p1_turn(1)
        q_turn(1)
        s2_multiply(1)
        p1_exp(3)
        v_widen(0, 3, "scalar")
        p1_reciprocal(2)
        v_widen(0, 6, "vector")
        p1_scale(2)
        p1_copy(1)
        q_copy(1)
        p1_turn(2)
        p1_quantize(0)
        p1_reciprocal(3)
        v_widen(0, 4, "vector")
        v_interleave(0, 0)
        p1_scale(3)
        p1_copy(2)
        p1_turn(3)
        v_interleave(0, 1)
        widen_step(-2, "vector")
        p1_quantize(1)
        v_copy(0, 0)
        s2_max(0)
        p1_copy(3)
        v_quantize(0, 0)
        s2_shift(0)
        s2_exp(0)
        p1_quantize(2)
        p1_quantize(3)
        widen_step(-2, "scalar")
        v_copy(0, 1)
        nc.scalar.copy(
            out=g2_all[:].rearrange("p (u h e) -> p u h e", u=2, e=2),
            in_=g2_plain[:].rearrange("p (h u e) -> p u h e", u=2, e=2),
        )
        t_multiply(0, 0)

        for k in range(STEPS + OUT_LAG):
            b, i = divmod(k, PAIRS)
            chunk, chunk_before, chunk_after = chunk_of(k), chunk_of(k - 1), chunk_of(k + 1)
            a_half = (b + 1, i - 1) if i in (1, 2) and b + 1 < B else None
            ready = k - OUT_LAG
            if i == 0 and b + 2 < B:
                load_a(b + 2)
                load_q(b + 2, 0)
                load_q(b + 2, 1)
                load_v(b + 2)
            if k < STEPS:
                s2_max(2 * k + 1)
            if 1 <= k <= STEPS:
                p2_scale(2 * k - 1)
            if i == 3 and b + 1 < B:
                a_quantize(b + 1)
            if a_half:
                a_turn(*a_half)
            if 1 <= k <= STEPS:
                p2_turn(k - 1)
            if k + 2 < STEPS:
                q_turn(k + 2)
            if 1 <= k < STEPS:
                s2_exp(2 * k)
            if k < STEPS:
                s2_shift(2 * k + 1)
            if chunk and k >= 1:
                v_copy(*chunk)
            if k < STEPS:
                s2_exp(2 * k + 1)
            if a_half:
                a_copy(*a_half, nc.scalar.copy)
            widen_step(k, "scalar")
            if 1 <= k <= STEPS:
                p2_copy(k - 1)
            if k + 2 < STEPS:
                q_copy(k + 2)
            if chunk_before:
                u_scale(*chunk_before)
            if k + 1 < STEPS:
                q_quantize(k + 1)
            if k >= 1:
                widen_step(k - 1, "vector")
            if 2 <= k <= STEPS + 1:
                p2_quantize(k - 2)
            if k < STEPS:
                p2_reciprocal(2 * k)
            if chunk_before:
                u_quantize(*chunk_before)
            if chunk:
                v_quantize(*chunk)
            if k < STEPS:
                p2_scale(2 * k)
            if k + 1 < STEPS:
                s2_multiply(2 * k + 2)
                s2_multiply(2 * k + 3)
                s2_max(2 * k + 2)
            if k < STEPS:
                p2_reciprocal(2 * k + 1)
            if ready >= 0:
                out_multiply(ready)
            if chunk:
                t_multiply(*chunk)
            if chunk_after:
                v_interleave(*chunk_after)
            if ready >= 0:
                out_copy(ready, 0, nc.scalar.copy)
            if k + 1 < STEPS:
                s2_shift(2 * k + 2)
            if ready >= 0:
                if k < STEPS:
                    out_copy(ready, 1, nc.scalar.copy)
                    out_store(ready, [(0, 2)])
                else:
                    out_copy(ready, 1, nc.vector.tensor_copy)
                    out_store(ready, [(0, 1), (1, 2)])
